import numpy as np
import ml_dtypes


def mxq(x, axis, fmt="e4m3"):
    dtype, down = {"e4m3": (ml_dtypes.float8_e4m3fn, 7), "e5m2": (ml_dtypes.float8_e5m2, 14)}[fmt]
    v = np.moveaxis(np.asarray(x, np.float32).astype(ml_dtypes.bfloat16).astype(np.float64), axis, -1)
    blocks = v.reshape(v.shape[:-1] + (-1, 32))
    amax = np.abs(blocks).max(-1, keepdims=True)
    byte = np.maximum(np.where(amax > 0, np.frexp(amax)[1] - 1 + 127, 0) - down, 1)
    scale = np.exp2(byte - 127.0)
    codes = (blocks / scale).astype(np.float32).astype(dtype).astype(np.float64)
    return np.moveaxis((codes * scale).reshape(v.shape), -1, axis)


WIDE = False


def mx_kscale(k):
    if not WIDE:
        return np.ones(k)
    levels = np.array([10, -10, 5, -5, 0])
    if k % 512:
        return np.exp2(np.random.permutation(np.resize(levels, k // 32))).repeat(32)
    a = np.empty((k // 512, 16))
    for p in range(k // 512):
        a[p, :8] = np.random.permutation(np.resize(levels, 8))
        for g in range(8):
            far = levels[np.abs(levels - a[p, g]) >= 10]
            a[p, g + 8] = far[np.random.randint(len(far))]
    return np.exp2(a.ravel()).repeat(32)


BF16 = ml_dtypes.bfloat16


def bf(x):
    return np.asarray(x, np.float32).astype(BF16)


def f64(x):
    return np.asarray(x).astype(np.float64)

def planes(Y):
    n, m = Y.shape
    b = f64(bf(Y)).reshape(n // 32, 32, m)
    amax = np.abs(b).max(1)
    byte = np.clip(np.where(amax > 0, np.frexp(amax)[1] - 1 + 127 - 7, 1), 1, 254)
    codes = (b * np.exp2(127.0 - byte)[:, None, :]).reshape(n, m).astype(np.float32).astype(ml_dtypes.float8_e4m3fn).view(np.uint8)
    words = codes.reshape(n // 512, 128, 4, m).transpose(0, 1, 3, 2)
    return np.ascontiguousarray(words), np.ascontiguousarray(byte.astype(np.uint8).reshape(n // 512, 16, m))


M, N, D, C = 1024, 2048, 512, 512


def setup_inputs():
    s, t = mx_kscale(D), mx_kscale(N)
    y = np.random.standard_normal((M, D)) / np.sqrt(D) * s[None, :]
    x = np.random.standard_normal((N, D)) / s[None, :]
    b = 0.4 * np.random.standard_normal(M)
    o = np.log(M) + 0.7 * np.random.standard_normal(N)
    g = np.random.standard_normal(N) * t
    z = np.random.standard_normal((N, C)) / t[:, None]
    v = np.random.standard_normal((M, C))
    return {"y": bf(y), "x": bf(x), "b": bf(b), "o": bf(o), "g": bf(g), "z": bf(z), "v": bf(v)}


def centroid_posterior(logits, outlier):
    e = np.exp(logits)
    den = np.exp(outlier) + np.sum(e, axis=0)
    return logits.shape[0] * e / den[None, :]


def core(y, x, b, o, g, z, v):
    n_points = x.shape[0]
    l = (mxq(f64(y), 1, "e4m3") @ mxq(f64(x), 1, "e4m3").T) + f64(b)[:, None]
    p = centroid_posterior(l, f64(o))
    mass = np.mean(p, axis=1)
    q = p * f64(g)[None, :]
    t = (mxq(q, 1, "e4m3") @ mxq(f64(z), 0, "e4m3")) / np.sqrt(n_points)
    return t - mass[:, None] * f64(v)


def reference(y, x, b, o, g, z, v):
    R_out = core(y, x, b, o, g, z, v)
    words, scales = planes(R_out.T)
    return R_out, words, scales

@@ -1,0 +1,490 @@
+import math
+from contextlib import ExitStack
+
+import concourse.mybir as mybir
+from concourse.masks import make_identity
+
+M, N, D, C = 1024, 2048, 512, 512
+FLOPS = 2 * M * N * D + 2 * M * N * C
+
+F32 = mybir.dt.float32
+BF16 = mybir.dt.bfloat16
+I32 = mybir.dt.int32
+U32 = mybir.dt.uint32
+U8 = mybir.dt.uint8
+FP8X4 = mybir.dt.float8_e4m3fn_x4
+ALU = mybir.AluOpType
+ACT = mybir.ActivationFunctionType
+AX = mybir.AxisListType
+
+P = 128
+PACK = 4
+GROUPS = N // (P * PACK)
+TILES = GROUPS * PACK
+M_TILES = M // P
+HALF = 512
+CHUNK = 256
+CHUNKS = M // CHUNK
+ROW = M + 8
+TEMPER = 8.0
+SHIFT_PER_BIT = -TEMPER * math.log(2.0) / 2.0**23
+SHIFT_BASE = TEMPER * 127.0 * math.log(2.0) + 0.5 * TEMPER * math.log(M + 1.0)
+
+
+def tile_centroidposteriorgainmassdifference_kernel(tc, y, x, b, o, g, z, v, out_0, out_1, out_2):
+    nc = tc.nc
+    with ExitStack() as ctx:
+        keep = ctx.enter_context(tc.tile_pool(name="keep", bufs=1))
+        ring2 = ctx.enter_context(tc.tile_pool(name="ring2", bufs=2))
+        ring3 = ctx.enter_context(tc.tile_pool(name="ring3", bufs=3))
+        ring4 = ctx.enter_context(tc.tile_pool(name="ring4", bufs=4))
+        psum = ctx.enter_context(tc.psum_pool(name="psum", bufs=1))
+        ctx.enter_context(tc.manual_schedule())
+
+        def bank(k):
+            return psum.tile([P, HALF], F32, name="bank%d" % k, tag="bank%d" % k)
+
+        def kept(name, shape, dtype):
+            return keep.tile(shape, dtype, name=name, tag=name, align_bytes=64)
+
+        ident = kept("ident", [P, P], F32)
+        ones = kept("ones", [P, P], BF16)
+        b_row = kept("b_row", [P, M], BF16)
+        b_all = kept("b_all", [P, M], BF16)
+        warm = kept("warm", [P, 1], F32)
+        o_sb = kept("o_sb", [P, GROUPS, PACK], BF16)
+        g_sb = kept("g_sb", [P, GROUPS, PACK], BF16)
+        gain = kept("gain", [P, TILES], F32)
+        soft_sum = kept("soft_sum", [P, TILES], F32)
+        shift = kept("shift", [P, TILES], F32)
+        den = kept("den", [P, TILES], F32)
+        inv_den = kept("inv_den", [P, TILES, 2], F32)
+        factor = kept("factor", [P, TILES], F32)
+        mass_sum = kept("mass_sum", [P, M_TILES], F32)
+        mass = kept("mass", [P, M_TILES], F32)
+        x_raw = [kept("x_raw%d" % k, [P, 2, D], BF16) for k in range(2 * GROUPS)]
+        y_raw = [kept("y_raw%d" % h, [P, 4, D], BF16) for h in range(2)]
+        z_raw = [kept("z_raw%d" % k, [P, PACK, C], BF16) for k in range(GROUPS)]
+        v_raw = kept("v_raw", [P, M_TILES, C], BF16)
+        x_codes = kept("x_codes", [P, N], U32)
+        x_scales = kept("x_scales", [P, N], U8)
+        y_codes = kept("y_codes", [P, M], U32)
+        y_scales = kept("y_scales", [P, M], U8)
+        z_codes = kept("z_codes", [P, GROUPS, C], U32)
+        z_scales = kept("z_scales", [P, GROUPS, C], U8)
+        q_codes = kept("q_codes", [P, GROUPS, M], U32)
+        q_scales = kept("q_scales", [P, GROUPS, M], U8)
+        r_codes = kept("r_codes", [P, M], U32)
+        r_scales = kept("r_scales", [P, M], U8)
+
+        x_view = x.rearrange("(g p t) d -> g p t d", p=P, t=PACK)
+        y_view = y.rearrange("(a p) d -> p a d", p=P)
+        z_view = z.rearrange("(g p t) c -> g p t c", p=P, t=PACK)
+
+        def load_x(k):
+            nc.sync.dma_start(out=x_raw[k][:], in_=x_view[k // 2, :, 2 * (k % 2) : 2 * (k % 2) + 2, :])
+
+        def load_z(k):
+            nc.sync.dma_start(out=z_raw[k][:], in_=z_view[k])
+
+        nc.vector.memset(b_row[:].bitcast(I32), 0)
+        nc.vector.memset(ones[:], 1.0)
+        make_identity(nc, ident[:])
+        nc.scalar.dma_start(out=b_row[0:1, :], in_=b.rearrange("(r m) -> r m", r=1))
+        nc.scalar.activation(out=warm[:], in_=ones[:, 0:1], func=ACT.Exp)
+        load_x(0)
+        for h in range(2):
+            nc.sync.dma_start(out=y_raw[h][:], in_=y_view[:, 4 * h : 4 * h + 4, :])
+        load_x(1)
+        nc.sync.dma_start(out=o_sb[:], in_=o.rearrange("(g p t) -> p g t", p=P, t=PACK))
+        nc.sync.dma_start(out=g_sb[:], in_=g.rearrange("(g p t) -> p g t", p=P, t=PACK))
+        load_x(2)
+        load_x(3)
+        load_z(0)
+        load_x(4)
+        load_x(5)
+        load_z(1)
+        load_x(6)
+        load_x(7)
+        load_z(2)
+        load_z(3)
+        nc.sync.dma_start(out=v_raw[:], in_=v.rearrange("(a p) c -> p a c", p=P))
+
+        turned = {}
+        staged = {}
+
+        def turn(key, rows, k):
+            acc = bank(k)
+            for a in range(2):
+                words = rows[:, a, :].bitcast(F32)
+                for u in range(2):
+                    s = 2 * a + u
+                    nc.tensor.transpose(acc[:, s * P : (s + 1) * P], words[:, u : 2 * P : 2], ident[:])
+            turned[key] = acc
+
+        def spill(key, engine):
+            stage = ring4.tile([P, 4 * CHUNK], BF16, name="stage", tag="stage", align_bytes=64)
+            dst = stage[:].bitcast(F32).rearrange("p (a r u) -> p a r u", a=2, u=2)
+            src = turned[key][:].rearrange("p (a u r) -> p a r u", a=2, u=2)
+            if engine == "scalar":
+                nc.scalar.copy(out=dst, in_=src)
+            else:
+                nc.vector.tensor_copy(out=dst, in_=src)
+            staged[key] = stage
+
+        def quantize(src, codes, scales):
+            nc.vector.quantize_mx(out=codes.bitcast(FP8X4), scales=scales, in_=src)
+
+        def quantize_x(k):
+            cols = slice(k * CHUNK, (k + 1) * CHUNK)
+            quantize(staged[("x", k)][:], x_codes[:, cols], x_scales[:, cols])
+
+        def quantize_y(k):
+            cols = slice(k * CHUNK, (k + 1) * CHUNK)
+            quantize(staged[("y", k)][:], y_codes[:, cols], y_scales[:, cols])
+
+        def y_rows(k):
+            return y_raw[k // 2][:, 2 * (k % 2) : 2 * (k % 2) + 2, :]
+
+        z_stage = {}
+
+        def weave_z(k):
+            stage = ring2.tile([P, C, PACK], BF16, name="z_stage", tag="z_stage", align_bytes=64)
+            for s in range(2):
+                cols = slice(s * CHUNK, (s + 1) * CHUNK)
+                nc.gpsimd.tensor_scalar(
+                    out=stage[:, cols, :].rearrange("p (c i) t -> p c t i", i=4),
+                    in0=z_raw[k][:, :, cols].rearrange("p t (c i) -> p c t i", i=4),
+                    scalar1=1.0,
+                    scalar2=0.0,
+                    op0=ALU.mult,
+                    op1=ALU.add,
+                )
+            z_stage[k] = stage
+
+        def quantize_z(k):
+            quantize(z_stage[k][:].rearrange("p c t -> p (c t)"), z_codes[:, k, :], z_scales[:, k, :])
+
+        scores = {}
+        logits = {}
+        q_stage = {}
+        accs = {}
+
+        def score(i, h):
+            acc = bank((2 * i + h) % 3)
+            rows = slice(i * P, (i + 1) * P)
+            cols = slice(h * HALF, (h + 1) * HALF)
+            nc.tensor.matmul_mx(
+                out=acc[:],
+                lhsT=x_codes[:, rows].bitcast(FP8X4),
+                lhsT_scale=x_scales[:, rows],
+                rhs=y_codes[:, cols].bitcast(FP8X4),
+                rhs_scale=y_scales[:, cols],
+                start=True,
+                stop=True,
+            )
+            scores[(i, h)] = acc
+
+        def open_group(k):
+            rows = ring3.tile([P, PACK, ROW], F32, name="logits", tag="logits", align_bytes=64)
+            nc.vector.tensor_copy(out=rows[:, :, M : M + 1], in_=o_sb[:, k, :].unsqueeze(2))
+            logits[k] = rows
+
+        def add_bias(i, h):
+            cols = slice(h * HALF, (h + 1) * HALF)
+            nc.vector.tensor_tensor(
+                out=logits[i // PACK][:, i % PACK, cols], in0=scores[(i, h)][:], in1=b_all[:, cols], op=ALU.add
+            )
+
+        def soft_exp(i):
+            junk = ring2.tile([P, M + 1], BF16, name="junk", tag="junk")
+            nc.scalar.activation(
+                out=junk[:],
+                in_=logits[i // PACK][:, i % PACK, 0 : M + 1],
+                func=ACT.Exp,
+                scale=1.0 / TEMPER,
+                accum_out=soft_sum[:, i : i + 1],
+            )
+
+        def make_shift(i):
+            nc.scalar.activation(
+                out=shift[:, i : i + 1],
+                in_=soft_sum[:, i : i + 1].bitcast(U32),
+                func=ACT.Copy,
+                scale=SHIFT_PER_BIT,
+                bias=SHIFT_BASE,
+            )
+
+        def exp_tile(i):
+            row = logits[i // PACK][:, i % PACK, 0 : M + 1]
+            nc.scalar.activation(
+                out=row, in_=row, func=ACT.Exp, bias=shift[:, i : i + 1], accum_out=den[:, i : i + 1]
+            )
+
+        def invert(i):
+            nc.vector.reciprocal(out=inv_den[:, i, :], in_=den[:, i : i + 1].to_broadcast([P, 2]))
+
+        def make_factor(k):
+            cols = slice(k * PACK, (k + 1) * PACK)
+            nc.vector.tensor_tensor(out=factor[:, cols], in0=inv_den[:, cols, 0], in1=gain[:, cols], op=ALU.mult)
+
+        def mass_terms(i, tiles):
+            for j in tiles:
+                nc.tensor.matmul(
+                    out=mass_view[:, j, i, :],
+                    lhsT=logits[i // PACK][:, i % PACK, j * P : (j + 1) * P],
+                    rhs=inv_den[:, i, :],
+                    start=True,
+                    stop=True,
+                )
+
+        def weave_q(k, s):
+            stage = ring3.tile([P, CHUNK, PACK], BF16, name="q_stage", tag="q_stage", align_bytes=64)
+            nc.vector.tensor_tensor(
+                out=stage[:].rearrange("p (c i) t -> p c t i", i=2),
+                in0=logits[k][:, :, s * CHUNK : (s + 1) * CHUNK].rearrange("p t (c i) -> p c t i", i=2),
+                in1=factor[:, k * PACK : (k + 1) * PACK].unsqueeze(1).unsqueeze(3).to_broadcast([P, CHUNK // 2, PACK, 2]),
+                op=ALU.mult,
+            )
+            q_stage[(k, s)] = stage
+
+        def quantize_q(k, s):
+            cols = slice(s * CHUNK, (s + 1) * CHUNK)
+            quantize(q_stage[(k, s)][:].rearrange("p m t -> p (m t)"), q_codes[:, k, cols], q_scales[:, k, cols])
+
+        def gather(j, k):
+            if k == 0:
+                accs[j] = bank([4, 5, 6, 7, 2, 0, 1, 3][j])
+            rows = slice(j * P, (j + 1) * P)
+            nc.tensor.matmul_mx(
+                out=accs[j][:],
+                lhsT=q_codes[:, k, rows].bitcast(FP8X4),
+                lhsT_scale=q_scales[:, k, rows],
+                rhs=z_codes[:, k, :].bitcast(FP8X4),
+                rhs_scale=z_scales[:, k, :],
+                start=(k == 0),
+                stop=(k == GROUPS - 1),
+            )
+
+        turn(("x", 0), x_raw[0], 4)
+        turn(("y", 0), y_rows(0), 5)
+        turn(("y", 1), y_rows(1), 6)
+        b_banks = []
+        for h in range(2):
+            acc = bank(h)
+            nc.tensor.matmul(out=acc[:], lhsT=ones[:], rhs=b_row[:, h * HALF : (h + 1) * HALF], start=True, stop=True)
+            b_banks.append(acc)
+        turn(("y", 2), y_rows(2), 2)
+        turn(("y", 3), y_rows(3), 3)
+        turn(("x", 1), x_raw[1], 7)
+        spill(("x", 0), "scalar")
+        spill(("y", 0), "vector")
+        spill(("y", 1), "scalar")
+        quantize_x(0)
+        quantize_y(0)
+        nc.vector.tensor_copy(out=b_all[:, 0:HALF], in_=b_banks[0][:])
+        quantize_y(1)
+        nc.scalar.copy(out=b_all[:, HALF:M], in_=b_banks[1][:])
+        spill(("y", 2), "scalar")
+        spill(("y", 3), "vector")
+        quantize_y(2)
+        open_group(0)
+        quantize_y(3)
+        spill(("x", 1), "scalar")
+        score(0, 0)
+        score(0, 1)
+        weave_z(0)
+        weave_z(1)
+
+        mass_bank = bank(3)
+        mass_view = mass_bank[:, 0 : M_TILES * TILES * 2].rearrange("p (j i e) -> p j i e", j=M_TILES, e=2)
+
+        for i in range(TILES):
+            if i + 1 < TILES:
+                score(i + 1, 0)
+            add_bias(i, 0)
+            if i < 6:
+                turn(("x", i + 2), x_raw[i + 2], 4 + i % 4)
+            if i + 1 < TILES:
+                score(i + 1, 1)
+            add_bias(i, 1)
+            soft_exp(i)
+            if i >= 1:
+                exp_tile(i - 1)
+            make_shift(i)
+            if i == 0:
+                nc.vector.tensor_scalar(
+                    out=gain[:], in0=g_sb[:].rearrange("p g t -> p (g t)"), scalar1=float(M), scalar2=None, op0=ALU.mult
+                )
+            if i < 7:
+                quantize_x(i + 1)
+            if i >= 6:
+                weave_q((i - 6) // 4, (i - 6) % 4)
+            if i >= 2:
+                invert(i - 2)
+            if i < 6:
+                spill(("x", i + 2), "vector")
+            if 2 <= i < 6:
+                quantize_z(i - 2)
+                if i < GROUPS:
+                    weave_z(i)
+            if i >= 6:
+                quantize_q((i - 6) // 4, (i - 6) % 4)
+            if i >= 2:
+                mass_terms(i - 2, range(0, 4))
+            if i >= 7:
+                gather((i - 7) % 4, (i - 7) // 4)
+            if i >= 2:
+                mass_terms(i - 2, range(4, 8))
+            if i >= 2 and (i - 2) % 4 == 3:
+                make_factor((i - 2) // 4)
+            if i % 4 == 2 and i // 4 + 1 < GROUPS:
+                open_group(i // 4 + 1)
+
+        exp_tile(15)
+        gather(1, 2)
+        gather(4, 0)
+        gather(4, 1)
+        gather(2, 2)
+        gather(3, 2)
+        for j in (5, 6):
+            gather(j, 0)
+            gather(j, 1)
+        weave_q(2, 2)
+        invert(14)
+        quantize_q(2, 2)
+        mass_terms(14, range(8))
+        gather(4, 2)
+        gather(5, 2)
+        weave_q(2, 3)
+        invert(15)
+        mass_terms(15, range(8))
+        quantize_q(2, 3)
+        gather(6, 2)
+        make_factor(3)
+        weave_q(3, 0)
+        nc.vector.tensor_reduce(
+            out=mass_sum[:], in_=mass_view.rearrange("p j i e -> p j (i e)"), axis=AX.X, op=ALU.add
+        )
+        quantize_q(3, 0)
+        nc.vector.tensor_scalar(out=mass[:], in0=mass_sum[:], scalar1=M / (2.0 * N), scalar2=None, op0=ALU.mult)
+
+        weighted = {}
+        results = {}
+        rounded = {}
+        r_turned = {}
+        r_stage = {}
+
+        def weigh(j):
+            t = ring4.tile([P, C], F32, name="weighted", tag="weighted")
+            nc.scalar.activation(out=t[:], in_=v_raw[:, j, :], func=ACT.Copy, scale=mass[:, j : j + 1])
+            weighted[j] = t
+
+        def finish(j):
+            t = ring4.tile([P, C], F32, name="result", tag="result", bufs=M_TILES)
+            nc.vector.scalar_tensor_tensor(
+                out=t[:], in0=accs[j][:], scalar=1.0 / math.sqrt(N), in1=weighted[j][:], op0=ALU.mult, op1=ALU.subtract
+            )
+            nc.sync.dma_start(out=out_0[j * P : (j + 1) * P, :], in_=t[:])
+            results[j] = t
+
+        def round_result(j):
+            t = ring3.tile([P, C], BF16, name="rounded", tag="rounded", align_bytes=64)
+            nc.scalar.copy(
+                out=t[:].rearrange("p (u j e) -> p u j e", u=2, e=2),
+                in_=results[j][:].rearrange("p (j u e) -> p u j e", u=2, e=2),
+            )
+            rounded[j] = t
+
+        def turn_result(j):
+            acc = bank([4, 5, 6, 7, 2, 0, 1, 3][j])
+            words = rounded[j][:].bitcast(F32)
+            for u in range(2):
+                nc.tensor.transpose(acc[:, u * P : (u + 1) * P], words[:, u * P : (u + 1) * P], ident[:])
+            r_turned[j] = acc
+
+        def spill_result(j):
+            t = ring3.tile([P, C], BF16, name="r_stage", tag="r_stage", align_bytes=64)
+            nc.scalar.copy(
+                out=t[:].bitcast(F32).rearrange("p (r u) -> p r u", u=2),
+                in_=r_turned[j][:, 0 : 2 * P].rearrange("p (u r) -> p r u", u=2),
+            )
+            r_stage[j] = t
+
+        words_out = out_1[0].rearrange("p m t -> p (m t)").bitcast(I32)
+
+        def quantize_result(j):
+            cols = slice(j * P, (j + 1) * P)
+            quantize(r_stage[j][:], r_codes[:, cols], r_scales[:, cols])
+            if j % 2 == 1:
+                pair = slice((j - 1) * P, (j + 1) * P)
+                nc.sync.dma_start(out=words_out[:, pair], in_=r_codes[:, pair].bitcast(I32))
+
+        gather(0, 3)
+        gather(1, 3)
+        for k in range(3):
+            gather(7, k)
+        weigh(0)
+        weigh(1)
+        weigh(2)
+        weave_q(3, 1)
+        finish(0)
+        quantize_q(3, 1)
+        gather(2, 3)
+        gather(3, 3)
+        round_result(0)
+        weigh(3)
+        finish(1)
+        round_result(1)
+        turn_result(0)
+        weave_q(3, 2)
+        finish(2)
+        weigh(4)
+        spill_result(0)
+        quantize_q(3, 2)
+        gather(4, 3)
+        gather(5, 3)
+        turn_result(1)
+        round_result(2)
+        finish(3)
+        weigh(5)
+        spill_result(1)
+        round_result(3)
+        turn_result(2)
+        weave_q(3, 3)
+        quantize_result(0)
+        quantize_q(3, 3)
+        gather(6, 3)
+        gather(7, 3)
+        turn_result(3)
+        finish(4)
+        weigh(6)
+        spill_result(2)
+        round_result(4)
+        quantize_result(1)
+        finish(5)
+        weigh(7)
+        spill_result(3)
+        round_result(5)
+        turn_result(4)
+        quantize_result(2)
+        finish(6)
+        quantize_result(3)
+        spill_result(4)
+        round_result(6)
+        turn_result(5)
+        finish(7)
+        spill_result(5)
+        round_result(7)
+        turn_result(6)
+        turn_result(7)
+        quantize_result(4)
+        quantize_result(5)
+        spill_result(6)
+        spill_result(7)
+        quantize_result(6)
+        quantize_result(7)
+        scales_out = out_2[0].bitcast(I32)
+        for s in range(4):
+            queue = nc.scalar if s % 2 else nc.sync
+            queue.dma_start(out=scales_out[4 * s : 4 * s + 4, :], in_=r_scales[32 * s : 32 * s + 4, :].bitcast(I32))

@@ -26,6 +26,7 @@ HALF = 512
 CHUNK = 256
 CHUNKS = M // CHUNK
 ROW = M + 8
+ACC_BANK = [5, 6, 7, 2, 0, 1, 3, 4]
 TEMPER = 8.0
 SHIFT_PER_BIT = -TEMPER * math.log(2.0) / 2.0**23
 SHIFT_BASE = TEMPER * 127.0 * math.log(2.0) + 0.5 * TEMPER * math.log(M + 1.0)
@@ -58,7 +59,7 @@ def tile_centroidposteriorgainmassdifference_kernel(tc, y, x, b, o, g, z, v, out
         soft_sum = kept("soft_sum", [P, TILES], F32)
         shift = kept("shift", [P, TILES], F32)
         den = kept("den", [P, TILES], F32)
-        inv_den = kept("inv_den", [P, TILES, 2], F32)
+        inv_den = kept("inv_den", [P, TILES], F32)
         factor = kept("factor", [P, TILES], F32)
         mass_sum = kept("mass_sum", [P, M_TILES], F32)
         mass = kept("mass", [P, M_TILES], F32)
@@ -98,16 +99,11 @@ def tile_centroidposteriorgainmassdifference_kernel(tc, y, x, b, o, g, z, v, out
         load_x(1)
         nc.sync.dma_start(out=o_sb[:], in_=o.rearrange("(g p t) -> p g t", p=P, t=PACK))
         nc.sync.dma_start(out=g_sb[:], in_=g.rearrange("(g p t) -> p g t", p=P, t=PACK))
-        load_x(2)
-        load_x(3)
-        load_z(0)
-        load_x(4)
-        load_x(5)
-        load_z(1)
+        for k in range(GROUPS):
+            load_x(2 + k)
+            load_z(k)
         load_x(6)
         load_x(7)
-        load_z(2)
-        load_z(3)
         nc.sync.dma_start(out=v_raw[:], in_=v.rearrange("(a p) c -> p a c", p=P))
 
         turned = {}
@@ -148,19 +144,28 @@ def tile_centroidposteriorgainmassdifference_kernel(tc, y, x, b, o, g, z, v, out
 
         z_stage = {}
 
+        def open_z(k):
+            z_stage[k] = ring3.tile([P, C, PACK], BF16, name="z_stage", tag="z_stage", align_bytes=64)
+
         def weave_z(k):
-            stage = ring2.tile([P, C, PACK], BF16, name="z_stage", tag="z_stage", align_bytes=64)
+            open_z(k)
             for s in range(2):
                 cols = slice(s * CHUNK, (s + 1) * CHUNK)
                 nc.gpsimd.tensor_scalar(
-                    out=stage[:, cols, :].rearrange("p (c i) t -> p c t i", i=4),
-                    in0=z_raw[k][:, :, cols].rearrange("p t (c i) -> p c t i", i=4),
+                    out=z_stage[k][:, cols, :],
+                    in0=z_raw[k][:, :, cols].rearrange("p t c -> p c t"),
                     scalar1=1.0,
                     scalar2=0.0,
                     op0=ALU.mult,
                     op1=ALU.add,
                 )
-            z_stage[k] = stage
+
+        def weave_z_piece(k, s):
+            cols = slice(s * 64, (s + 1) * 64)
+            nc.scalar.copy(
+                out=z_stage[k][:, cols, :].rearrange("p (c i) t -> p c t i", i=4),
+                in_=z_raw[k][:, :, cols].rearrange("p t (c i) -> p c t i", i=4),
+            )
 
         def quantize_z(k):
             quantize(z_stage[k][:].rearrange("p c t -> p (c t)"), z_codes[:, k, :], z_scales[:, k, :])
@@ -222,21 +227,49 @@ def tile_centroidposteriorgainmassdifference_kernel(tc, y, x, b, o, g, z, v, out
             )
 
         def invert(i):
-            nc.vector.reciprocal(out=inv_den[:, i, :], in_=den[:, i : i + 1].to_broadcast([P, 2]))
+            nc.vector.reciprocal(out=inv_den[:, i : i + 1], in_=den[:, i : i + 1])
 
         def make_factor(k):
             cols = slice(k * PACK, (k + 1) * PACK)
-            nc.vector.tensor_tensor(out=factor[:, cols], in0=inv_den[:, cols, 0], in1=gain[:, cols], op=ALU.mult)
+            nc.vector.tensor_tensor(out=factor[:, cols], in0=inv_den[:, cols], in1=gain[:, cols], op=ALU.mult)
 
-        def mass_terms(i, tiles):
-            for j in tiles:
+        posterior = {}
+
+        def normalise(i, engine):
+            t = ring3.tile([P, M], F32, name="posterior", tag="posterior")
+            row = logits[i // PACK][:, i % PACK, 0:M]
+            w = inv_den[:, i : i + 1]
+            if engine == "scalar":
+                nc.scalar.activation(out=t[:], in_=row, func=ACT.Copy, scale=w)
+            elif engine == "vector":
+                nc.vector.tensor_scalar(out=t[:], in0=row, scalar1=w, scalar2=None, op0=ALU.mult)
+            else:
+                nc.gpsimd.tensor_scalar(out=t[:], in0=row, scalar1=w, scalar2=0.0, op0=ALU.mult, op1=ALU.add)
+            posterior[i] = t
+
+        def mass_terms(i, h):
+            for s in range(4):
+                j = 4 * h + s
                 nc.tensor.matmul(
-                    out=mass_view[:, j, i, :],
-                    lhsT=logits[i // PACK][:, i % PACK, j * P : (j + 1) * P],
-                    rhs=inv_den[:, i, :],
-                    start=True,
-                    stop=True,
+                    out=mass_banks[h][:, s * P : (s + 1) * P],
+                    lhsT=posterior[i][:, j * P : (j + 1) * P],
+                    rhs=ident[:],
+                    is_transpose=True,
+                    start=(i == 0 and s == 0),
+                    stop=(i == TILES - 1 and s == 3),
                 )
+
+        def sum_mass(h):
+            nc.vector.tensor_reduce(
+                out=mass_sum[:, 4 * h : 4 * h + 4],
+                in_=mass_banks[h][:].rearrange("p (s r) -> p s r", s=4),
+                axis=AX.X,
+                op=ALU.add,
+            )
+
+        def scale_mass(h):
+            cols = slice(4 * h, 4 * h + 4)
+            nc.vector.tensor_scalar(out=mass[:, cols], in0=mass_sum[:, cols], scalar1=M / N, scalar2=None, op0=ALU.mult)
 
         def weave_q(k, s):
             stage = ring3.tile([P, CHUNK, PACK], BF16, name="q_stage", tag="q_stage", align_bytes=64)
@@ -254,7 +287,7 @@ def tile_centroidposteriorgainmassdifference_kernel(tc, y, x, b, o, g, z, v, out
 
         def gather(j, k):
             if k == 0:
-                accs[j] = bank([4, 5, 6, 7, 2, 0, 1, 3][j])
+                accs[j] = bank(ACC_BANK[j])
             rows = slice(j * P, (j + 1) * P)
             nc.tensor.matmul_mx(
                 out=accs[j][:],
@@ -293,81 +326,90 @@ def tile_centroidposteriorgainmassdifference_kernel(tc, y, x, b, o, g, z, v, out
         spill(("x", 1), "scalar")
         score(0, 0)
         score(0, 1)
-        weave_z(0)
-        weave_z(1)
+        for k in range(3):
+            weave_z(k)
 
-        mass_bank = bank(3)
-        mass_view = mass_bank[:, 0 : M_TILES * TILES * 2].rearrange("p (j i e) -> p j i e", j=M_TILES, e=2)
+        mass_banks = [bank(3), bank(4)]
 
         for i in range(TILES):
             if i + 1 < TILES:
                 score(i + 1, 0)
             add_bias(i, 0)
             if i < 6:
-                turn(("x", i + 2), x_raw[i + 2], 4 + i % 4)
+                turn(("x", i + 2), x_raw[i + 2], 5 + i % 3)
+            if i >= 3:
+                mass_terms(i - 3, 0)
             if i + 1 < TILES:
                 score(i + 1, 1)
+            if i >= 3:
+                mass_terms(i - 3, 1)
+            if i >= 8 and i % 4 < 3:
+                gather(i % 4, (i - 8) // 4)
             add_bias(i, 1)
             soft_exp(i)
             if i >= 1:
                 exp_tile(i - 1)
             make_shift(i)
+            if i == 7:
+                open_z(3)
+            if 7 <= i < 15:
+                weave_z_piece(3, i - 7)
             if i == 0:
                 nc.vector.tensor_scalar(
                     out=gain[:], in0=g_sb[:].rearrange("p g t -> p (g t)"), scalar1=float(M), scalar2=None, op0=ALU.mult
                 )
-            if i < 7:
-                quantize_x(i + 1)
-            if i >= 6:
-                weave_q((i - 6) // 4, (i - 6) % 4)
-            if i >= 2:
-                invert(i - 2)
             if i < 6:
                 spill(("x", i + 2), "vector")
-            if 2 <= i < 6:
+            if i >= 6 and i % 4 == 2:
+                make_factor((i - 6) // 4)
+            if i < 7:
+                quantize_x(i + 1)
+            if 2 <= i < 5:
                 quantize_z(i - 2)
-                if i < GROUPS:
-                    weave_z(i)
-            if i >= 6:
-                quantize_q((i - 6) // 4, (i - 6) % 4)
-            if i >= 2:
-                mass_terms(i - 2, range(0, 4))
             if i >= 7:
-                gather((i - 7) % 4, (i - 7) // 4)
-            if i >= 2:
-                mass_terms(i - 2, range(4, 8))
-            if i >= 2 and (i - 2) % 4 == 3:
-                make_factor((i - 2) // 4)
-            if i % 4 == 2 and i // 4 + 1 < GROUPS:
+                quantize_q((i - 7) // 4, (i - 7) % 4)
+            if i % 4 == 3 and i // 4 + 1 < GROUPS:
                 open_group(i // 4 + 1)
+            if i >= 2:
+                invert(i - 2)
+            if i >= 6:
+                weave_q((i - 6) // 4, (i - 6) % 4)
+            if 2 <= i < TILES - 1:
+                normalise(i - 2, "gpsimd")
 
         exp_tile(15)
-        gather(1, 2)
-        gather(4, 0)
-        gather(4, 1)
-        gather(2, 2)
-        gather(3, 2)
-        for j in (5, 6):
+        for j in (3, 4, 5):
             gather(j, 0)
             gather(j, 1)
-        weave_q(2, 2)
+        gather(0, 2)
+        gather(1, 2)
+        normalise(13, "vector")
+        mass_terms(13, 0)
+        mass_terms(13, 1)
+        quantize_q(2, 1)
+        gather(2, 2)
+        gather(3, 2)
         invert(14)
+        normalise(14, "scalar")
+        weave_q(2, 2)
+        quantize_z(3)
         quantize_q(2, 2)
-        mass_terms(14, range(8))
-        gather(4, 2)
-        gather(5, 2)
+        mass_terms(14, 0)
+        mass_terms(14, 1)
         weave_q(2, 3)
         invert(15)
-        mass_terms(15, range(8))
+        normalise(15, "scalar")
+        gather(4, 2)
+        gather(5, 2)
+        mass_terms(15, 0)
+        mass_terms(15, 1)
         quantize_q(2, 3)
-        gather(6, 2)
         make_factor(3)
         weave_q(3, 0)
-        nc.vector.tensor_reduce(
-            out=mass_sum[:], in_=mass_view.rearrange("p j i e -> p j (i e)"), axis=AX.X, op=ALU.add
-        )
+        sum_mass(0)
         quantize_q(3, 0)
-        nc.vector.tensor_scalar(out=mass[:], in0=mass_sum[:], scalar1=M / (2.0 * N), scalar2=None, op0=ALU.mult)
+        scale_mass(0)
+        sum_mass(1)
 
         weighted = {}
         results = {}
@@ -397,7 +439,7 @@ def tile_centroidposteriorgainmassdifference_kernel(tc, y, x, b, o, g, z, v, out
             rounded[j] = t
 
         def turn_result(j):
-            acc = bank([4, 5, 6, 7, 2, 0, 1, 3][j])
+            acc = bank(ACC_BANK[j])
             words = rounded[j][:].bitcast(F32)
             for u in range(2):
                 nc.tensor.transpose(acc[:, u * P : (u + 1) * P], words[:, u * P : (u + 1) * P], ident[:])
@@ -423,15 +465,18 @@ def tile_centroidposteriorgainmassdifference_kernel(tc, y, x, b, o, g, z, v, out
         gather(0, 3)
         gather(1, 3)
         for k in range(3):
-            gather(7, k)
+            gather(6, k)
         weigh(0)
         weigh(1)
         weigh(2)
         weave_q(3, 1)
-        finish(0)
+        scale_mass(1)
         quantize_q(3, 1)
         gather(2, 3)
         gather(3, 3)
+        for k in range(3):
+            gather(7, k)
+        finish(0)
         round_result(0)
         weigh(3)
         finish(1)

@@ -15,7 +15,6 @@ U8 = mybir.dt.uint8
 FP8X4 = mybir.dt.float8_e4m3fn_x4
 ALU = mybir.AluOpType
 ACT = mybir.ActivationFunctionType
-AX = mybir.AxisListType
 
 P = 128
 PACK = 4
@@ -26,7 +25,8 @@ HALF = 512
 CHUNK = 256
 CHUNKS = M // CHUNK
 ROW = M + 8
-ACC_BANK = [5, 6, 7, 2, 0, 1, 3, 4]
+ACC_BANK = [5, 6, 7, 0, 1, 2, 3, 4]
+ROUND_ON_VECTOR = (5, 6, 7)
 TEMPER = 8.0
 SHIFT_PER_BIT = -TEMPER * math.log(2.0) / 2.0**23
 SHIFT_BASE = TEMPER * 127.0 * math.log(2.0) + 0.5 * TEMPER * math.log(M + 1.0)
@@ -49,7 +49,7 @@ def tile_centroidposteriorgainmassdifference_kernel(tc, y, x, b, o, g, z, v, out
             return keep.tile(shape, dtype, name=name, tag=name, align_bytes=64)
 
         ident = kept("ident", [P, P], F32)
-        ones = kept("ones", [P, P], BF16)
+        ones = kept("ones", [P, HALF], BF16)
         b_row = kept("b_row", [P, M], BF16)
         b_all = kept("b_all", [P, M], BF16)
         warm = kept("warm", [P, 1], F32)
@@ -61,10 +61,9 @@ def tile_centroidposteriorgainmassdifference_kernel(tc, y, x, b, o, g, z, v, out
         den = kept("den", [P, TILES], F32)
         inv_den = kept("inv_den", [P, TILES], F32)
         factor = kept("factor", [P, TILES], F32)
-        mass_sum = kept("mass_sum", [P, M_TILES], F32)
         mass = kept("mass", [P, M_TILES], F32)
         x_raw = [kept("x_raw%d" % k, [P, 2, D], BF16) for k in range(2 * GROUPS)]
-        y_raw = [kept("y_raw%d" % h, [P, 4, D], BF16) for h in range(2)]
+        y_raw = [kept("y_raw%d" % k, [P, 2, D], BF16) for k in range(4)]
         z_raw = [kept("z_raw%d" % k, [P, PACK, C], BF16) for k in range(GROUPS)]
         v_raw = kept("v_raw", [P, M_TILES, C], BF16)
         x_codes = kept("x_codes", [P, N], U32)
@@ -88,18 +87,20 @@ def tile_centroidposteriorgainmassdifference_kernel(tc, y, x, b, o, g, z, v, out
         def load_z(k):
             nc.sync.dma_start(out=z_raw[k][:], in_=z_view[k])
 
-        nc.vector.memset(b_row[:].bitcast(I32), 0)
         nc.vector.memset(ones[:], 1.0)
+        nc.gpsimd.memset(b_row[:].bitcast(I32), 0)
         make_identity(nc, ident[:])
         nc.scalar.dma_start(out=b_row[0:1, :], in_=b.rearrange("(r m) -> r m", r=1))
         nc.scalar.activation(out=warm[:], in_=ones[:, 0:1], func=ACT.Exp)
         load_x(0)
-        for h in range(2):
-            nc.sync.dma_start(out=y_raw[h][:], in_=y_view[:, 4 * h : 4 * h + 4, :])
+        for k in range(4):
+            nc.sync.dma_start(out=y_raw[k][:], in_=y_view[:, 2 * k : 2 * k + 2, :])
         load_x(1)
+        load_x(2)
+        load_z(0)
         nc.sync.dma_start(out=o_sb[:], in_=o.rearrange("(g p t) -> p g t", p=P, t=PACK))
         nc.sync.dma_start(out=g_sb[:], in_=g.rearrange("(g p t) -> p g t", p=P, t=PACK))
-        for k in range(GROUPS):
+        for k in range(1, GROUPS):
             load_x(2 + k)
             load_z(k)
         load_x(6)
@@ -139,18 +140,18 @@ def tile_centroidposteriorgainmassdifference_kernel(tc, y, x, b, o, g, z, v, out
             cols = slice(k * CHUNK, (k + 1) * CHUNK)
             quantize(staged[("y", k)][:], y_codes[:, cols], y_scales[:, cols])
 
-        def y_rows(k):
-            return y_raw[k // 2][:, 2 * (k % 2) : 2 * (k % 2) + 2, :]
+        def keep_warm(acc, count):
+            for repeat in range(count):
+                nc.tensor.matmul(out=acc[:], lhsT=ones[:, 0:P], rhs=ones[:], start=True, stop=True)
 
         z_stage = {}
 
         def open_z(k):
             z_stage[k] = ring3.tile([P, C, PACK], BF16, name="z_stage", tag="z_stage", align_bytes=64)
 
-        def weave_z(k):
-            open_z(k)
-            for s in range(2):
-                cols = slice(s * CHUNK, (s + 1) * CHUNK)
+        def weave_z(k, first, count, engine):
+            cols = slice(first * 64, (first + count) * 64)
+            if engine == "gpsimd":
                 nc.gpsimd.tensor_scalar(
                     out=z_stage[k][:, cols, :],
                     in0=z_raw[k][:, :, cols].rearrange("p t c -> p c t"),
@@ -159,13 +160,13 @@ def tile_centroidposteriorgainmassdifference_kernel(tc, y, x, b, o, g, z, v, out
                     op0=ALU.mult,
                     op1=ALU.add,
                 )
-
-        def weave_z_piece(k, s):
-            cols = slice(s * 64, (s + 1) * 64)
-            nc.scalar.copy(
-                out=z_stage[k][:, cols, :].rearrange("p (c i) t -> p c t i", i=4),
-                in_=z_raw[k][:, :, cols].rearrange("p t (c i) -> p c t i", i=4),
-            )
+                return
+            dst = z_stage[k][:, cols, :].rearrange("p (c i) t -> p c t i", i=4)
+            src = z_raw[k][:, :, cols].rearrange("p t (c i) -> p c t i", i=4)
+            if engine == "scalar":
+                nc.scalar.copy(out=dst, in_=src)
+            else:
+                nc.vector.tensor_copy(out=dst, in_=src)
 
         def quantize_z(k):
             quantize(z_stage[k][:].rearrange("p c t -> p (c t)"), z_codes[:, k, :], z_scales[:, k, :])
@@ -176,7 +177,7 @@ def tile_centroidposteriorgainmassdifference_kernel(tc, y, x, b, o, g, z, v, out
         accs = {}
 
         def score(i, h):
-            acc = bank((2 * i + h) % 3)
+            acc = bank(h)
             rows = slice(i * P, (i + 1) * P)
             cols = slice(h * HALF, (h + 1) * HALF)
             nc.tensor.matmul_mx(
@@ -192,7 +193,7 @@ def tile_centroidposteriorgainmassdifference_kernel(tc, y, x, b, o, g, z, v, out
 
         def open_group(k):
             rows = ring3.tile([P, PACK, ROW], F32, name="logits", tag="logits", align_bytes=64)
-            nc.vector.tensor_copy(out=rows[:, :, M : M + 1], in_=o_sb[:, k, :].unsqueeze(2))
+            nc.scalar.copy(out=rows[:, :, M : M + 1], in_=o_sb[:, k, :].unsqueeze(2))
             logits[k] = rows
 
         def add_bias(i, h):
@@ -231,7 +232,7 @@ def tile_centroidposteriorgainmassdifference_kernel(tc, y, x, b, o, g, z, v, out
 
         def make_factor(k):
             cols = slice(k * PACK, (k + 1) * PACK)
-            nc.vector.tensor_tensor(out=factor[:, cols], in0=inv_den[:, cols], in1=gain[:, cols], op=ALU.mult)
+            nc.vector.tensor_tensor(out=factor[:, cols], in0=inv_den[:, cols], in1=gain_bank[:, cols], op=ALU.mult)
 
         posterior = {}
 
@@ -259,27 +260,38 @@ def tile_centroidposteriorgainmassdifference_kernel(tc, y, x, b, o, g, z, v, out
                     stop=(i == TILES - 1 and s == 3),
                 )
 
-        def sum_mass(h):
-            nc.vector.tensor_reduce(
-                out=mass_sum[:, 4 * h : 4 * h + 4],
-                in_=mass_banks[h][:].rearrange("p (s r) -> p s r", s=4),
-                axis=AX.X,
-                op=ALU.add,
+        def sum_mass(j):
+            unread = ring2.tile([P, P], BF16, name="unread", tag="unread")
+            nc.scalar.activation(
+                out=unread[:],
+                in_=mass_banks[j // 4][:, (j % 4) * P : (j % 4 + 1) * P],
+                func=ACT.Copy,
+                scale=M / N,
+                accum_out=mass[:, j : j + 1],
             )
 
-        def scale_mass(h):
-            cols = slice(4 * h, 4 * h + 4)
-            nc.vector.tensor_scalar(out=mass[:, cols], in0=mass_sum[:, cols], scalar1=M / N, scalar2=None, op0=ALU.mult)
+        def spread_factor(k):
+            cols = slice(k * PACK, (k + 1) * PACK)
+            nc.tensor.matmul(out=factor_bank[:, cols], lhsT=ident[:], rhs=factor[:, cols], start=True, stop=True)
 
-        def weave_q(k, s):
-            stage = ring3.tile([P, CHUNK, PACK], BF16, name="q_stage", tag="q_stage", align_bytes=64)
+        def open_q(k, s):
+            q_stage[(k, s)] = ring4.tile([P, CHUNK, PACK], BF16, name="q_stage", tag="q_stage", align_bytes=64)
+
+        def weave_q(k, s, width):
             nc.vector.tensor_tensor(
-                out=stage[:].rearrange("p (c i) t -> p c t i", i=2),
-                in0=logits[k][:, :, s * CHUNK : (s + 1) * CHUNK].rearrange("p t (c i) -> p c t i", i=2),
-                in1=factor[:, k * PACK : (k + 1) * PACK].unsqueeze(1).unsqueeze(3).to_broadcast([P, CHUNK // 2, PACK, 2]),
+                out=q_stage[(k, s)][:, 0:width, :].rearrange("p (c i) t -> p c t i", i=2),
+                in0=logits[k][:, :, s * CHUNK : s * CHUNK + width].rearrange("p t (c i) -> p c t i", i=2),
+                in1=factor_bank[:, k * PACK : (k + 1) * PACK].unsqueeze(1).unsqueeze(3).to_broadcast([P, width // 2, PACK, 2]),
                 op=ALU.mult,
             )
-            q_stage[(k, s)] = stage
+
+        def weave_q_rest(k, s, first):
+            nc.gpsimd.tensor_tensor(
+                out=q_stage[(k, s)][:, first:CHUNK, :],
+                in0=logits[k][:, :, s * CHUNK + first : (s + 1) * CHUNK].rearrange("p t m -> p m t"),
+                in1=factor[:, k * PACK : (k + 1) * PACK].unsqueeze(1).to_broadcast([P, CHUNK - first, PACK]),
+                op=ALU.mult,
+            )
 
         def quantize_q(k, s):
             cols = slice(s * CHUNK, (s + 1) * CHUNK)
@@ -299,117 +311,133 @@ def tile_centroidposteriorgainmassdifference_kernel(tc, y, x, b, o, g, z, v, out
                 stop=(k == GROUPS - 1),
             )
 
-        turn(("x", 0), x_raw[0], 4)
-        turn(("y", 0), y_rows(0), 5)
-        turn(("y", 1), y_rows(1), 6)
+        factor_bank = bank(4)
+        gain_bank = factor_bank[:, TILES : 2 * TILES]
+        keep_warm(factor_bank, 4)
+        turn(("x", 0), x_raw[0], 5)
+        turn(("y", 0), y_raw[0], 6)
         b_banks = []
         for h in range(2):
             acc = bank(h)
-            nc.tensor.matmul(out=acc[:], lhsT=ones[:], rhs=b_row[:, h * HALF : (h + 1) * HALF], start=True, stop=True)
+            nc.tensor.matmul(out=acc[:], lhsT=ones[:, 0:P], rhs=b_row[:, h * HALF : (h + 1) * HALF], start=True, stop=True)
             b_banks.append(acc)
-        turn(("y", 2), y_rows(2), 2)
-        turn(("y", 3), y_rows(3), 3)
-        turn(("x", 1), x_raw[1], 7)
+            turn(("y", 1 + h), y_raw[1 + h], [7, 2][h])
+        turn(("y", 3), y_raw[3], 3)
         spill(("x", 0), "scalar")
+        keep_warm(factor_bank, 1)
+        turn(("x", 1), x_raw[1], 5)
         spill(("y", 0), "vector")
-        spill(("y", 1), "scalar")
         quantize_x(0)
+        nc.scalar.copy(out=b_all[:, 0:HALF], in_=b_banks[0][:])
         quantize_y(0)
-        nc.vector.tensor_copy(out=b_all[:, 0:HALF], in_=b_banks[0][:])
-        quantize_y(1)
+        spill(("y", 1), "vector")
         nc.scalar.copy(out=b_all[:, HALF:M], in_=b_banks[1][:])
         spill(("y", 2), "scalar")
-        spill(("y", 3), "vector")
+        quantize_y(1)
+        score(0, 0)
+        turn(("x", 2), x_raw[2], 6)
+        spill(("y", 3), "scalar")
         quantize_y(2)
         open_group(0)
         quantize_y(3)
         spill(("x", 1), "scalar")
-        score(0, 0)
         score(0, 1)
-        for k in range(3):
-            weave_z(k)
+        nc.scalar.activation(out=gain[:], in_=g_sb[:].rearrange("p g t -> p (g t)"), func=ACT.Copy, scale=float(M))
+        for k in (0, 1, 3):
+            open_z(k)
+        for s in range(8):
+            weave_z(0, s, 1, "gpsimd")
 
-        mass_banks = [bank(3), bank(4)]
+        mass_banks = [bank(2), bank(3)]
 
         for i in range(TILES):
-            if i + 1 < TILES:
-                score(i + 1, 0)
-            add_bias(i, 0)
-            if i < 6:
-                turn(("x", i + 2), x_raw[i + 2], 5 + i % 3)
+            if i >= 6 and i % 4 == 2:
+                spread_factor((i - 6) // 4)
+            for h in range(2):
+                add_bias(i, h)
+                if i + 1 < TILES:
+                    score(i + 1, h)
+            if i < 5:
+                turn(("x", i + 3), x_raw[i + 3], 5 + (i + 2) % 3)
             if i >= 3:
                 mass_terms(i - 3, 0)
-            if i + 1 < TILES:
-                score(i + 1, 1)
-            if i >= 3:
                 mass_terms(i - 3, 1)
             if i >= 8 and i % 4 < 3:
                 gather(i % 4, (i - 8) // 4)
-            add_bias(i, 1)
+            if i < 4:
+                keep_warm(factor_bank, 1)
+            if i == 3:
+                nc.tensor.matmul(out=gain_bank, lhsT=ident[:], rhs=gain[:], start=True, stop=True)
+            if 4 <= i < 8:
+                keep_warm(bank(6), 1)
             soft_exp(i)
             if i >= 1:
                 exp_tile(i - 1)
             make_shift(i)
-            if i == 7:
-                open_z(3)
-            if 7 <= i < 15:
-                weave_z_piece(3, i - 7)
-            if i == 0:
-                nc.vector.tensor_scalar(
-                    out=gain[:], in0=g_sb[:].rearrange("p g t -> p (g t)"), scalar1=float(M), scalar2=None, op0=ALU.mult
-                )
-            if i < 6:
-                spill(("x", i + 2), "vector")
-            if i >= 6 and i % 4 == 2:
-                make_factor((i - 6) // 4)
+            if i % 4 == 2 and i // 4 + 1 < GROUPS:
+                open_group(i // 4 + 1)
             if i < 7:
                 quantize_x(i + 1)
-            if 2 <= i < 5:
-                quantize_z(i - 2)
+            if i in (2, 10, 12):
+                quantize_z({2: 0, 10: 1, 12: 2}[i])
+            if i == 4:
+                weave_z(3, 6, 2, "vector")
+                open_z(2)
+            if i in (5, 6):
+                weave_z(2, 2 * (i - 5), 2, "vector")
+            if 7 <= i < 11:
+                weave_z(2, i - 3, 1, "scalar")
             if i >= 7:
                 quantize_q((i - 7) // 4, (i - 7) % 4)
-            if i % 4 == 3 and i // 4 + 1 < GROUPS:
-                open_group(i // 4 + 1)
             if i >= 2:
                 invert(i - 2)
-            if i >= 6:
-                weave_q((i - 6) // 4, (i - 6) % 4)
-            if 2 <= i < TILES - 1:
                 normalise(i - 2, "gpsimd")
+            if i >= 2:
+                weave_z(1 if i < 10 else 3, (i - 2) % 8, 1, "gpsimd")
+            if i < 6:
+                spill(("x", i + 2), "vector")
+            if i >= 6:
+                k, s = divmod(i - 6, 4)
+                open_q(k, s)
+                weave_q(k, s, CHUNK)
+            if i >= 5 and i % 4 == 1:
+                make_factor((i - 5) // 4)
 
         exp_tile(15)
-        for j in (3, 4, 5):
+        for j in (3, 4):
             gather(j, 0)
             gather(j, 1)
         gather(0, 2)
         gather(1, 2)
-        normalise(13, "vector")
         mass_terms(13, 0)
         mass_terms(13, 1)
+        open_q(2, 2)
+        weave_q(2, 2, CHUNK)
+        invert(14)
+        normalise(14, "gpsimd")
         quantize_q(2, 1)
         gather(2, 2)
         gather(3, 2)
-        invert(14)
-        normalise(14, "scalar")
-        weave_q(2, 2)
-        quantize_z(3)
-        quantize_q(2, 2)
-        mass_terms(14, 0)
-        mass_terms(14, 1)
-        weave_q(2, 3)
+        open_q(2, 3)
+        weave_q(2, 3, CHUNK)
         invert(15)
         normalise(15, "scalar")
+        quantize_z(3)
+        make_factor(3)
+        quantize_q(2, 2)
+        quantize_q(2, 3)
+        mass_terms(14, 0)
+        mass_terms(14, 1)
+        spread_factor(3)
         gather(4, 2)
-        gather(5, 2)
         mass_terms(15, 0)
         mass_terms(15, 1)
-        quantize_q(2, 3)
-        make_factor(3)
-        weave_q(3, 0)
-        sum_mass(0)
-        quantize_q(3, 0)
-        scale_mass(0)
-        sum_mass(1)
+        open_q(3, 3)
+        weave_q_rest(3, 3, 0)
+        open_q(3, 0)
+        weave_q(3, 0, CHUNK)
+        for j in range(M_TILES):
+            sum_mass(j)
 
         weighted = {}
         results = {}
@@ -419,7 +447,12 @@ def tile_centroidposteriorgainmassdifference_kernel(tc, y, x, b, o, g, z, v, out
 
         def weigh(j):
             t = ring4.tile([P, C], F32, name="weighted", tag="weighted")
-            nc.scalar.activation(out=t[:], in_=v_raw[:, j, :], func=ACT.Copy, scale=mass[:, j : j + 1])
+            if j < 4:
+                nc.scalar.activation(out=t[:], in_=v_raw[:, j, :], func=ACT.Copy, scale=mass[:, j : j + 1])
+            else:
+                nc.gpsimd.tensor_scalar(
+                    out=t[:], in0=v_raw[:, j, :], scalar1=mass[:, j : j + 1], scalar2=0.0, op0=ALU.mult, op1=ALU.add
+                )
             weighted[j] = t
 
         def finish(j):
@@ -431,11 +464,13 @@ def tile_centroidposteriorgainmassdifference_kernel(tc, y, x, b, o, g, z, v, out
             results[j] = t
 
         def round_result(j):
-            t = ring3.tile([P, C], BF16, name="rounded", tag="rounded", align_bytes=64)
-            nc.scalar.copy(
-                out=t[:].rearrange("p (u j e) -> p u j e", u=2, e=2),
-                in_=results[j][:].rearrange("p (j u e) -> p u j e", u=2, e=2),
-            )
+            t = ring4.tile([P, C], BF16, name="rounded", tag="rounded", align_bytes=64)
+            dst = t[:].rearrange("p (u j e) -> p u j e", u=2, e=2)
+            src = results[j][:].rearrange("p (j u e) -> p u j e", u=2, e=2)
+            if j in ROUND_ON_VECTOR:
+                nc.vector.tensor_copy(out=dst, in_=src)
+            else:
+                nc.scalar.copy(out=dst, in_=src)
             rounded[j] = t
 
         def turn_result(j):
@@ -446,7 +481,7 @@ def tile_centroidposteriorgainmassdifference_kernel(tc, y, x, b, o, g, z, v, out
             r_turned[j] = acc
 
         def spill_result(j):
-            t = ring3.tile([P, C], BF16, name="r_stage", tag="r_stage", align_bytes=64)
+            t = ring4.tile([P, C], BF16, name="r_stage", tag="r_stage", align_bytes=64, bufs=M_TILES)
             nc.scalar.copy(
                 out=t[:].bitcast(F32).rearrange("p (r u) -> p r u", u=2),
                 in_=r_turned[j][:, 0 : 2 * P].rearrange("p (u r) -> p r u", u=2),
@@ -462,73 +497,46 @@ def tile_centroidposteriorgainmassdifference_kernel(tc, y, x, b, o, g, z, v, out
                 pair = slice((j - 1) * P, (j + 1) * P)
                 nc.sync.dma_start(out=words_out[:, pair], in_=r_codes[:, pair].bitcast(I32))
 
+        for j in range(4):
+            weigh(j)
+        for k in range(3):
+            gather(5, k)
+        open_q(3, 1)
+        weave_q(3, 1, CHUNK)
+        quantize_q(3, 0)
         gather(0, 3)
         gather(1, 3)
         for k in range(3):
             gather(6, k)
-        weigh(0)
-        weigh(1)
-        weigh(2)
-        weave_q(3, 1)
-        scale_mass(1)
+        quantize_q(3, 3)
         quantize_q(3, 1)
         gather(2, 3)
         gather(3, 3)
-        for k in range(3):
-            gather(7, k)
+        gather(6, 3)
+        open_q(3, 2)
+        weave_q(3, 2, CHUNK)
         finish(0)
-        round_result(0)
-        weigh(3)
-        finish(1)
-        round_result(1)
-        turn_result(0)
-        weave_q(3, 2)
-        finish(2)
-        weigh(4)
-        spill_result(0)
         quantize_q(3, 2)
+        for k in range(4):
+            gather(7, k)
         gather(4, 3)
         gather(5, 3)
-        turn_result(1)
-        round_result(2)
-        finish(3)
-        weigh(5)
-        spill_result(1)
-        round_result(3)
-        turn_result(2)
-        weave_q(3, 3)
-        quantize_result(0)
-        quantize_q(3, 3)
-        gather(6, 3)
-        gather(7, 3)
-        turn_result(3)
-        finish(4)
-        weigh(6)
-        spill_result(2)
-        round_result(4)
-        quantize_result(1)
-        finish(5)
-        weigh(7)
-        spill_result(3)
-        round_result(5)
-        turn_result(4)
-        quantize_result(2)
-        finish(6)
-        quantize_result(3)
-        spill_result(4)
-        round_result(6)
-        turn_result(5)
-        finish(7)
-        spill_result(5)
-        round_result(7)
-        turn_result(6)
-        turn_result(7)
-        quantize_result(4)
-        quantize_result(5)
-        spill_result(6)
-        spill_result(7)
-        quantize_result(6)
-        quantize_result(7)
+        for j in range(1, M_TILES):
+            finish(j)
+            if j + 3 < M_TILES:
+                weigh(j + 3)
+            if j - 1 not in ROUND_ON_VECTOR:
+                round_result(j - 1)
+                turn_result(j - 1)
+            if j >= 4:
+                spill_result(j - 4)
+        for j in ROUND_ON_VECTOR:
+            round_result(j)
+            turn_result(j)
+        for j in range(M_TILES):
+            if j >= 4:
+                spill_result(j)
+            quantize_result(j)
         scales_out = out_2[0].bitcast(I32)
         for s in range(4):
             queue = nc.scalar if s % 2 else nc.sync

@@ -26,7 +26,16 @@ CHUNK = 256
 CHUNKS = M // CHUNK
 ROW = M + 8
 ACC_BANK = [5, 6, 7, 0, 1, 2, 3, 4]
-ROUND_ON_VECTOR = (5, 6, 7)
+ROUND_ON_VECTOR = (4, 5, 7)
+LEAD = [0, 0, 0, 0, 0, 1, 2] + [2] * 9
+SPILL_ON_SCALAR = {}
+MASS_AT = {3: (0,), 5: (1,), 6: (2, 3), **{i: (i - 3,) for i in range(7, TILES)}}
+PAIR_ORDER = [0, 1, 2, 3, 6, 5, 4, 7]
+FINISH_ORDER = [0, 1, 2, 3, 6, 4, 5, 7]
+LAST_SPLIT = 32
+THIRD_SPLIT = 128
+WEIGH_ON_SCALAR = (0, 1, 2, 3, 6)
+EARLY_INVERT = 7
 TEMPER = 8.0
 SHIFT_PER_BIT = -TEMPER * math.log(2.0) / 2.0**23
 SHIFT_BASE = TEMPER * 127.0 * math.log(2.0) + 0.5 * TEMPER * math.log(M + 1.0)
@@ -50,6 +59,7 @@ def tile_centroidposteriorgainmassdifference_kernel(tc, y, x, b, o, g, z, v, out
 
         ident = kept("ident", [P, P], F32)
         ones = kept("ones", [P, HALF], BF16)
+        zeros = kept("zeros", [P, P], BF16)
         b_row = kept("b_row", [P, M], BF16)
         b_all = kept("b_all", [P, M], BF16)
         warm = kept("warm", [P, 1], F32)
@@ -88,6 +98,7 @@ def tile_centroidposteriorgainmassdifference_kernel(tc, y, x, b, o, g, z, v, out
             nc.sync.dma_start(out=z_raw[k][:], in_=z_view[k])
 
         nc.vector.memset(ones[:], 1.0)
+        nc.vector.memset(zeros[:], 0.0)
         nc.gpsimd.memset(b_row[:].bitcast(I32), 0)
         make_identity(nc, ident[:])
         nc.scalar.dma_start(out=b_row[0:1, :], in_=b.rearrange("(r m) -> r m", r=1))
@@ -143,6 +154,9 @@ def tile_centroidposteriorgainmassdifference_kernel(tc, y, x, b, o, g, z, v, out
         def keep_warm(acc, count):
             for repeat in range(count):
                 nc.tensor.matmul(out=acc[:], lhsT=ones[:, 0:P], rhs=ones[:], start=True, stop=True)
+
+        def add_nothing(h):
+            nc.tensor.matmul(out=mass_banks[h][:], lhsT=zeros[:], rhs=ones[:], start=False, stop=False)
 
         z_stage = {}
 
@@ -227,8 +241,8 @@ def tile_centroidposteriorgainmassdifference_kernel(tc, y, x, b, o, g, z, v, out
                 out=row, in_=row, func=ACT.Exp, bias=shift[:, i : i + 1], accum_out=den[:, i : i + 1]
             )
 
-        def invert(i):
-            nc.vector.reciprocal(out=inv_den[:, i : i + 1], in_=den[:, i : i + 1])
+        def invert(i, count=1):
+            nc.vector.reciprocal(out=inv_den[:, i : i + count], in_=den[:, i : i + count])
 
         def make_factor(k):
             cols = slice(k * PACK, (k + 1) * PACK)
@@ -275,7 +289,7 @@ def tile_centroidposteriorgainmassdifference_kernel(tc, y, x, b, o, g, z, v, out
             nc.tensor.matmul(out=factor_bank[:, cols], lhsT=ident[:], rhs=factor[:, cols], start=True, stop=True)
 
         def open_q(k, s):
-            q_stage[(k, s)] = ring4.tile([P, CHUNK, PACK], BF16, name="q_stage", tag="q_stage", align_bytes=64)
+            q_stage[(k, s)] = ring3.tile([P, CHUNK, PACK], BF16, name="q_stage", tag="q_stage", align_bytes=64)
 
         def weave_q(k, s, width):
             nc.vector.tensor_tensor(
@@ -311,6 +325,15 @@ def tile_centroidposteriorgainmassdifference_kernel(tc, y, x, b, o, g, z, v, out
                 stop=(k == GROUPS - 1),
             )
 
+        def half(n):
+            if n >= 2 * TILES:
+                return
+            if n % 8 == 0 and n > 0:
+                open_group(n // 8)
+            add_bias(n // 2, n % 2)
+            if n + 2 < 2 * TILES:
+                score(n // 2 + 1, n % 2)
+
         factor_bank = bank(4)
         gain_bank = factor_bank[:, TILES : 2 * TILES]
         keep_warm(factor_bank, 4)
@@ -335,7 +358,7 @@ def tile_centroidposteriorgainmassdifference_kernel(tc, y, x, b, o, g, z, v, out
         spill(("y", 2), "scalar")
         quantize_y(1)
         score(0, 0)
-        turn(("x", 2), x_raw[2], 6)
+        keep_warm(factor_bank, 1)
         spill(("y", 3), "scalar")
         quantize_y(2)
         open_group(0)
@@ -343,58 +366,60 @@ def tile_centroidposteriorgainmassdifference_kernel(tc, y, x, b, o, g, z, v, out
         spill(("x", 1), "scalar")
         score(0, 1)
         nc.scalar.activation(out=gain[:], in_=g_sb[:].rearrange("p g t -> p (g t)"), func=ACT.Copy, scale=float(M))
-        for k in (0, 1, 3):
-            open_z(k)
-        for s in range(8):
-            weave_z(0, s, 1, "gpsimd")
+        open_z(0)
+        for s in range(4):
+            weave_z(0, 2 * s, 2, "gpsimd")
 
         mass_banks = [bank(2), bank(3)]
 
-        for i in range(TILES):
+        for i in range(TILES - 1):
             if i >= 6 and i % 4 == 2:
                 spread_factor((i - 6) // 4)
             for h in range(2):
-                add_bias(i, h)
-                if i + 1 < TILES:
-                    score(i + 1, h)
-            if i < 5:
-                turn(("x", i + 3), x_raw[i + 3], 5 + (i + 2) % 3)
-            if i >= 3:
-                mass_terms(i - 3, 0)
-                mass_terms(i - 3, 1)
-            if i >= 8 and i % 4 < 3:
-                gather(i % 4, (i - 8) // 4)
-            if i < 4:
-                keep_warm(factor_bank, 1)
-            if i == 3:
-                nc.tensor.matmul(out=gain_bank, lhsT=ident[:], rhs=gain[:], start=True, stop=True)
-            if 4 <= i < 8:
-                keep_warm(bank(6), 1)
+                half(2 * i + LEAD[i] + h)
+                if i == 0 and h == 0:
+                    turn(("x", 2), x_raw[2], 6)
             soft_exp(i)
             if i >= 1:
                 exp_tile(i - 1)
             make_shift(i)
-            if i % 4 == 2 and i // 4 + 1 < GROUPS:
-                open_group(i // 4 + 1)
-            if i < 7:
+            if i in (2, 9, 13):
+                quantize_z({2: 0, 9: 1, 13: 2}[i])
+            if i >= EARLY_INVERT:
+                invert(i - 2)
+            if i in SPILL_ON_SCALAR:
+                spill(("x", SPILL_ON_SCALAR[i]), "scalar")
+            if i < 7 and i + 1 not in SPILL_ON_SCALAR.values():
                 quantize_x(i + 1)
-            if i in (2, 10, 12):
-                quantize_z({2: 0, 10: 1, 12: 2}[i])
-            if i == 4:
-                weave_z(3, 6, 2, "vector")
-                open_z(2)
-            if i in (5, 6):
-                weave_z(2, 2 * (i - 5), 2, "vector")
-            if 7 <= i < 11:
-                weave_z(2, i - 3, 1, "scalar")
+            if i - 1 in SPILL_ON_SCALAR:
+                quantize_x(SPILL_ON_SCALAR[i - 1])
+            if LEAD[i + 1] > LEAD[i]:
+                half(2 * i + 2 + LEAD[i])
+            if i < 5:
+                turn(("x", i + 3), x_raw[i + 3], 5 + (i + 2) % 3)
+            for late in MASS_AT.get(i, ()):
+                mass_terms(late, 0)
+                mass_terms(late, 1)
+            if i >= 8 and i % 4 < 3:
+                gather(i % 4, (i - 8) // 4)
+            if i < 3:
+                keep_warm(factor_bank, 1)
+            if i == 2:
+                nc.tensor.matmul(out=gain_bank, lhsT=ident[:], rhs=gain[:], start=True, stop=True)
+            if i in (6, 7, 11, 14):
+                add_nothing(0)
             if i >= 7:
                 quantize_q((i - 7) // 4, (i - 7) % 4)
-            if i >= 2:
+            if 2 <= i < EARLY_INVERT:
                 invert(i - 2)
+            if i >= 2:
                 normalise(i - 2, "gpsimd")
             if i >= 2:
-                weave_z(1 if i < 10 else 3, (i - 2) % 8, 1, "gpsimd")
-            if i < 6:
+                first, count = (i - 2, 1) if i < 6 else (2 * i - 8, 2)
+                if first % 8 == 0:
+                    open_z(1 + first // 8)
+                weave_z(1 + first // 8, first % 8, count, "gpsimd")
+            if i < 6 and i + 2 not in SPILL_ON_SCALAR.values():
                 spill(("x", i + 2), "vector")
             if i >= 6:
                 k, s = divmod(i - 6, 4)
@@ -403,42 +428,60 @@ def tile_centroidposteriorgainmassdifference_kernel(tc, y, x, b, o, g, z, v, out
             if i >= 5 and i % 4 == 1:
                 make_factor((i - 5) // 4)
 
+        weave_z(3, 6, 1, "scalar")
+        soft_exp(15)
+        exp_tile(14)
+        make_shift(15)
+        weave_z(3, 7, 1, "scalar")
         exp_tile(15)
-        for j in (3, 4):
-            gather(j, 0)
-            gather(j, 1)
+        open_q(2, 1)
+        weave_q(2, 1, CHUNK)
+        gather(3, 0)
+        gather(3, 1)
+        add_nothing(0)
+        mass_terms(12, 0)
+        mass_terms(12, 1)
+        gather(4, 0)
+        gather(4, 1)
+        quantize_q(2, 0)
+        invert(13)
+        quantize_q(2, 1)
+        normalise(13, "gpsimd")
         gather(0, 2)
         gather(1, 2)
-        mass_terms(13, 0)
-        mass_terms(13, 1)
         open_q(2, 2)
         weave_q(2, 2, CHUNK)
         invert(14)
-        normalise(14, "gpsimd")
-        quantize_q(2, 1)
-        gather(2, 2)
-        gather(3, 2)
+        normalise(14, "scalar")
         open_q(2, 3)
         weave_q(2, 3, CHUNK)
+        add_nothing(0)
+        add_nothing(1)
+        mass_terms(13, 0)
+        mass_terms(13, 1)
+        gather(2, 2)
+        gather(3, 2)
         invert(15)
         normalise(15, "scalar")
         quantize_z(3)
         make_factor(3)
         quantize_q(2, 2)
         quantize_q(2, 3)
+        spread_factor(3)
         mass_terms(14, 0)
         mass_terms(14, 1)
-        spread_factor(3)
-        gather(4, 2)
+        add_nothing(1)
         mass_terms(15, 0)
         mass_terms(15, 1)
+        gather(4, 2)
         open_q(3, 3)
-        weave_q_rest(3, 3, 0)
-        open_q(3, 0)
-        weave_q(3, 0, CHUNK)
-        for j in range(M_TILES):
-            sum_mass(j)
+        weave_q_rest(3, 3, LAST_SPLIT)
+        for s in (0, 1):
+            open_q(3, s)
+            weave_q(3, s, CHUNK)
+        weave_q(3, 3, LAST_SPLIT)
 
+        pairs = {}
         weighted = {}
         results = {}
         rounded = {}
@@ -446,19 +489,22 @@ def tile_centroidposteriorgainmassdifference_kernel(tc, y, x, b, o, g, z, v, out
         r_stage = {}
 
         def weigh(j):
-            t = ring4.tile([P, C], F32, name="weighted", tag="weighted")
-            if j < 4:
-                nc.scalar.activation(out=t[:], in_=v_raw[:, j, :], func=ACT.Copy, scale=mass[:, j : j + 1])
+            n = PAIR_ORDER.index(j)
+            if n // 2 not in pairs:
+                pairs[n // 2] = ring3.tile([P, 2, C], F32, name="weighted", tag="posterior")
+            t = pairs[n // 2][:, n % 2, :]
+            if j in WEIGH_ON_SCALAR:
+                nc.scalar.activation(out=t, in_=v_raw[:, j, :], func=ACT.Copy, scale=mass[:, j : j + 1])
             else:
                 nc.gpsimd.tensor_scalar(
-                    out=t[:], in0=v_raw[:, j, :], scalar1=mass[:, j : j + 1], scalar2=0.0, op0=ALU.mult, op1=ALU.add
+                    out=t, in0=v_raw[:, j, :], scalar1=mass[:, j : j + 1], scalar2=0.0, op0=ALU.mult, op1=ALU.add
                 )
             weighted[j] = t
 
         def finish(j):
             t = ring4.tile([P, C], F32, name="result", tag="result", bufs=M_TILES)
             nc.vector.scalar_tensor_tensor(
-                out=t[:], in0=accs[j][:], scalar=1.0 / math.sqrt(N), in1=weighted[j][:], op0=ALU.mult, op1=ALU.subtract
+                out=t[:], in0=accs[j][:], scalar=1.0 / math.sqrt(N), in1=weighted[j], op0=ALU.mult, op1=ALU.subtract
             )
             nc.sync.dma_start(out=out_0[j * P : (j + 1) * P, :], in_=t[:])
             results[j] = t
@@ -497,44 +543,56 @@ def tile_centroidposteriorgainmassdifference_kernel(tc, y, x, b, o, g, z, v, out
                 pair = slice((j - 1) * P, (j + 1) * P)
                 nc.sync.dma_start(out=words_out[:, pair], in_=r_codes[:, pair].bitcast(I32))
 
-        for j in range(4):
+        for j in range(M_TILES):
+            sum_mass(j)
+        for j in WEIGH_ON_SCALAR:
             weigh(j)
-        for k in range(3):
-            gather(5, k)
-        open_q(3, 1)
-        weave_q(3, 1, CHUNK)
+        gather(5, 0)
+        gather(5, 1)
         quantize_q(3, 0)
         gather(0, 3)
         gather(1, 3)
-        for k in range(3):
-            gather(6, k)
+        gather(6, 0)
+        gather(6, 1)
         quantize_q(3, 3)
         quantize_q(3, 1)
         gather(2, 3)
         gather(3, 3)
+        gather(5, 2)
+        gather(6, 2)
         gather(6, 3)
         open_q(3, 2)
-        weave_q(3, 2, CHUNK)
+        weave_q_rest(3, 2, THIRD_SPLIT)
+        weave_q(3, 2, THIRD_SPLIT)
         finish(0)
+        finish(1)
+        for j in (4, 5, 7):
+            weigh(j)
+        gather(7, 0)
+        gather(7, 1)
+        round_result(0)
         quantize_q(3, 2)
-        for k in range(4):
-            gather(7, k)
+        finish(2)
+        gather(7, 2)
         gather(4, 3)
         gather(5, 3)
-        for j in range(1, M_TILES):
-            finish(j)
-            if j + 3 < M_TILES:
-                weigh(j + 3)
-            if j - 1 not in ROUND_ON_VECTOR:
-                round_result(j - 1)
-                turn_result(j - 1)
-            if j >= 4:
-                spill_result(j - 4)
+        gather(7, 3)
+        turn_result(0)
+        round_result(1)
+        turn_result(1)
+        for n in range(3, M_TILES):
+            finish(FINISH_ORDER[n])
+            j = FINISH_ORDER[n - 1]
+            if j not in ROUND_ON_VECTOR:
+                round_result(j)
+                turn_result(j)
+            if n >= 4:
+                spill_result(FINISH_ORDER[n - 4])
         for j in ROUND_ON_VECTOR:
             round_result(j)
             turn_result(j)
-        for j in range(M_TILES):
-            if j >= 4:
+        for n, j in enumerate(FINISH_ORDER):
+            if n >= 4:
                 spill_result(j)
             quantize_result(j)
         scales_out = out_2[0].bitcast(I32)

import math
from contextlib import ExitStack

import concourse.mybir as mybir
from concourse.masks import make_identity

M, N, D, C = 1024, 2048, 512, 512
FLOPS = 2 * M * N * D + 2 * M * N * C

F32 = mybir.dt.float32
BF16 = mybir.dt.bfloat16
I32 = mybir.dt.int32
U32 = mybir.dt.uint32
U8 = mybir.dt.uint8
FP8X4 = mybir.dt.float8_e4m3fn_x4
ALU = mybir.AluOpType
ACT = mybir.ActivationFunctionType

P = 128
PACK = 4
GROUPS = N // (P * PACK)
TILES = GROUPS * PACK
M_TILES = M // P
HALF = 512
CHUNK = 256
CHUNKS = M // CHUNK
ROW = M + 8
ACC_BANK = [5, 6, 7, 0, 1, 2, 3, 4]
ROUND_ON_VECTOR = (4, 5, 7)
LEAD = [0, 0, 0, 0, 0, 1, 2] + [2] * 9
SPILL_ON_SCALAR = {}
MASS_AT = {3: (0,), 5: (1,), 6: (2, 3), **{i: (i - 3,) for i in range(7, TILES)}}
PAIR_ORDER = [0, 1, 2, 3, 6, 5, 4, 7]
FINISH_ORDER = [0, 1, 2, 3, 6, 4, 5, 7]
LAST_SPLIT = 32
THIRD_SPLIT = 128
WEIGH_ON_SCALAR = (0, 1, 2, 3, 6)
EARLY_INVERT = 7
TEMPER = 8.0
SHIFT_PER_BIT = -TEMPER * math.log(2.0) / 2.0**23
SHIFT_BASE = TEMPER * 127.0 * math.log(2.0) + 0.5 * TEMPER * math.log(M + 1.0)


def tile_centroidposteriorgainmassdifference_kernel(tc, y, x, b, o, g, z, v, out_0, out_1, out_2):
    nc = tc.nc
    with ExitStack() as ctx:
        keep = ctx.enter_context(tc.tile_pool(name="keep", bufs=1))
        ring2 = ctx.enter_context(tc.tile_pool(name="ring2", bufs=2))
        ring3 = ctx.enter_context(tc.tile_pool(name="ring3", bufs=3))
        ring4 = ctx.enter_context(tc.tile_pool(name="ring4", bufs=4))
        psum = ctx.enter_context(tc.psum_pool(name="psum", bufs=1))
        ctx.enter_context(tc.manual_schedule())

        def bank(k):
            return psum.tile([P, HALF], F32, name="bank%d" % k, tag="bank%d" % k)

        def kept(name, shape, dtype):
            return keep.tile(shape, dtype, name=name, tag=name, align_bytes=64)

        ident = kept("ident", [P, P], F32)
        ones = kept("ones", [P, HALF], BF16)
        zeros = kept("zeros", [P, P], BF16)
        b_row = kept("b_row", [P, M], BF16)
        b_all = kept("b_all", [P, M], BF16)
        warm = kept("warm", [P, 1], F32)
        o_sb = kept("o_sb", [P, GROUPS, PACK], BF16)
        g_sb = kept("g_sb", [P, GROUPS, PACK], BF16)
        gain = kept("gain", [P, TILES], F32)
        soft_sum = kept("soft_sum", [P, TILES], F32)
        shift = kept("shift", [P, TILES], F32)
        den = kept("den", [P, TILES], F32)
        inv_den = kept("inv_den", [P, TILES], F32)
        factor = kept("factor", [P, TILES], F32)
        mass = kept("mass", [P, M_TILES], F32)
        x_raw = [kept("x_raw%d" % k, [P, 2, D], BF16) for k in range(2 * GROUPS)]
        y_raw = [kept("y_raw%d" % k, [P, 2, D], BF16) for k in range(4)]
        z_raw = [kept("z_raw%d" % k, [P, PACK, C], BF16) for k in range(GROUPS)]
        v_raw = kept("v_raw", [P, M_TILES, C], BF16)
        x_codes = kept("x_codes", [P, N], U32)
        x_scales = kept("x_scales", [P, N], U8)
        y_codes = kept("y_codes", [P, M], U32)
        y_scales = kept("y_scales", [P, M], U8)
        z_codes = kept("z_codes", [P, GROUPS, C], U32)
        z_scales = kept("z_scales", [P, GROUPS, C], U8)
        q_codes = kept("q_codes", [P, GROUPS, M], U32)
        q_scales = kept("q_scales", [P, GROUPS, M], U8)
        r_codes = kept("r_codes", [P, M], U32)
        r_scales = kept("r_scales", [P, M], U8)

        x_view = x.rearrange("(g p t) d -> g p t d", p=P, t=PACK)
        y_view = y.rearrange("(a p) d -> p a d", p=P)
        z_view = z.rearrange("(g p t) c -> g p t c", p=P, t=PACK)

        def load_x(k):
            nc.sync.dma_start(out=x_raw[k][:], in_=x_view[k // 2, :, 2 * (k % 2) : 2 * (k % 2) + 2, :])

        def load_z(k):
            nc.sync.dma_start(out=z_raw[k][:], in_=z_view[k])

        nc.vector.memset(ones[:], 1.0)
        nc.vector.memset(zeros[:], 0.0)
        nc.gpsimd.memset(b_row[:].bitcast(I32), 0)
        make_identity(nc, ident[:])
        nc.scalar.dma_start(out=b_row[0:1, :], in_=b.rearrange("(r m) -> r m", r=1))
        nc.scalar.activation(out=warm[:], in_=ones[:, 0:1], func=ACT.Exp)
        load_x(0)
        for k in range(4):
            nc.sync.dma_start(out=y_raw[k][:], in_=y_view[:, 2 * k : 2 * k + 2, :])
        load_x(1)
        load_x(2)
        load_z(0)
        nc.sync.dma_start(out=o_sb[:], in_=o.rearrange("(g p t) -> p g t", p=P, t=PACK))
        nc.sync.dma_start(out=g_sb[:], in_=g.rearrange("(g p t) -> p g t", p=P, t=PACK))
        for k in range(1, GROUPS):
            load_x(2 + k)
            load_z(k)
        load_x(6)
        load_x(7)
        nc.sync.dma_start(out=v_raw[:], in_=v.rearrange("(a p) c -> p a c", p=P))

        turned = {}
        staged = {}

        def turn(key, rows, k):
            acc = bank(k)
            for a in range(2):
                words = rows[:, a, :].bitcast(F32)
                for u in range(2):
                    s = 2 * a + u
                    nc.tensor.transpose(acc[:, s * P : (s + 1) * P], words[:, u : 2 * P : 2], ident[:])
            turned[key] = acc

        def spill(key, engine):
            stage = ring4.tile([P, 4 * CHUNK], BF16, name="stage", tag="stage", align_bytes=64)
            dst = stage[:].bitcast(F32).rearrange("p (a r u) -> p a r u", a=2, u=2)
            src = turned[key][:].rearrange("p (a u r) -> p a r u", a=2, u=2)
            if engine == "scalar":
                nc.scalar.copy(out=dst, in_=src)
            else:
                nc.vector.tensor_copy(out=dst, in_=src)
            staged[key] = stage

        def quantize(src, codes, scales):
            nc.vector.quantize_mx(out=codes.bitcast(FP8X4), scales=scales, in_=src)

        def quantize_x(k):
            cols = slice(k * CHUNK, (k + 1) * CHUNK)
            quantize(staged[("x", k)][:], x_codes[:, cols], x_scales[:, cols])

        def quantize_y(k):
            cols = slice(k * CHUNK, (k + 1) * CHUNK)
            quantize(staged[("y", k)][:], y_codes[:, cols], y_scales[:, cols])

        def keep_warm(acc, count):
            for repeat in range(count):
                nc.tensor.matmul(out=acc[:], lhsT=ones[:, 0:P], rhs=ones[:], start=True, stop=True)

        def add_nothing(h):
            nc.tensor.matmul(out=mass_banks[h][:], lhsT=zeros[:], rhs=ones[:], start=False, stop=False)

        z_stage = {}

        def open_z(k):
            z_stage[k] = ring3.tile([P, C, PACK], BF16, name="z_stage", tag="z_stage", align_bytes=64)

        def weave_z(k, first, count, engine):
            cols = slice(first * 64, (first + count) * 64)
            if engine == "gpsimd":
                nc.gpsimd.tensor_scalar(
                    out=z_stage[k][:, cols, :],
                    in0=z_raw[k][:, :, cols].rearrange("p t c -> p c t"),
                    scalar1=1.0,
                    scalar2=0.0,
                    op0=ALU.mult,
                    op1=ALU.add,
                )
                return
            dst = z_stage[k][:, cols, :].rearrange("p (c i) t -> p c t i", i=4)
            src = z_raw[k][:, :, cols].rearrange("p t (c i) -> p c t i", i=4)
            if engine == "scalar":
                nc.scalar.copy(out=dst, in_=src)
            else:
                nc.vector.tensor_copy(out=dst, in_=src)

        def quantize_z(k):
            quantize(z_stage[k][:].rearrange("p c t -> p (c t)"), z_codes[:, k, :], z_scales[:, k, :])

        scores = {}
        logits = {}
        q_stage = {}
        accs = {}

        def score(i, h):
            acc = bank(h)
            rows = slice(i * P, (i + 1) * P)
            cols = slice(h * HALF, (h + 1) * HALF)
            nc.tensor.matmul_mx(
                out=acc[:],
                lhsT=x_codes[:, rows].bitcast(FP8X4),
                lhsT_scale=x_scales[:, rows],
                rhs=y_codes[:, cols].bitcast(FP8X4),
                rhs_scale=y_scales[:, cols],
                start=True,
                stop=True,
            )
            scores[(i, h)] = acc

        def open_group(k):
            rows = ring3.tile([P, PACK, ROW], F32, name="logits", tag="logits", align_bytes=64)
            nc.scalar.copy(out=rows[:, :, M : M + 1], in_=o_sb[:, k, :].unsqueeze(2))
            logits[k] = rows

        def add_bias(i, h):
            cols = slice(h * HALF, (h + 1) * HALF)
            nc.vector.tensor_tensor(
                out=logits[i // PACK][:, i % PACK, cols], in0=scores[(i, h)][:], in1=b_all[:, cols], op=ALU.add
            )

        def soft_exp(i):
            junk = ring2.tile([P, M + 1], BF16, name="junk", tag="junk")
            nc.scalar.activation(
                out=junk[:],
                in_=logits[i // PACK][:, i % PACK, 0 : M + 1],
                func=ACT.Exp,
                scale=1.0 / TEMPER,
                accum_out=soft_sum[:, i : i + 1],
            )

        def make_shift(i):
            nc.scalar.activation(
                out=shift[:, i : i + 1],
                in_=soft_sum[:, i : i + 1].bitcast(U32),
                func=ACT.Copy,
                scale=SHIFT_PER_BIT,
                bias=SHIFT_BASE,
            )

        def exp_tile(i):
            row = logits[i // PACK][:, i % PACK, 0 : M + 1]
            nc.scalar.activation(
                out=row, in_=row, func=ACT.Exp, bias=shift[:, i : i + 1], accum_out=den[:, i : i + 1]
            )

        def invert(i, count=1):
            nc.vector.reciprocal(out=inv_den[:, i : i + count], in_=den[:, i : i + count])

        def make_factor(k):
            cols = slice(k * PACK, (k + 1) * PACK)
            nc.vector.tensor_tensor(out=factor[:, cols], in0=inv_den[:, cols], in1=gain_bank[:, cols], op=ALU.mult)

        posterior = {}

        def normalise(i, engine):
            t = ring3.tile([P, M], F32, name="posterior", tag="posterior")
            row = logits[i // PACK][:, i % PACK, 0:M]
            w = inv_den[:, i : i + 1]
            if engine == "scalar":
                nc.scalar.activation(out=t[:], in_=row, func=ACT.Copy, scale=w)
            elif engine == "vector":
                nc.vector.tensor_scalar(out=t[:], in0=row, scalar1=w, scalar2=None, op0=ALU.mult)
            else:
                nc.gpsimd.tensor_scalar(out=t[:], in0=row, scalar1=w, scalar2=0.0, op0=ALU.mult, op1=ALU.add)
            posterior[i] = t

        def mass_terms(i, h):
            for s in range(4):
                j = 4 * h + s
                nc.tensor.matmul(
                    out=mass_banks[h][:, s * P : (s + 1) * P],
                    lhsT=posterior[i][:, j * P : (j + 1) * P],
                    rhs=ident[:],
                    is_transpose=True,
                    start=(i == 0 and s == 0),
                    stop=(i == TILES - 1 and s == 3),
                )

        def sum_mass(j):
            unread = ring2.tile([P, P], BF16, name="unread", tag="unread")
            nc.scalar.activation(
                out=unread[:],
                in_=mass_banks[j // 4][:, (j % 4) * P : (j % 4 + 1) * P],
                func=ACT.Copy,
                scale=M / N,
                accum_out=mass[:, j : j + 1],
            )

        def spread_factor(k):
            cols = slice(k * PACK, (k + 1) * PACK)
            nc.tensor.matmul(out=factor_bank[:, cols], lhsT=ident[:], rhs=factor[:, cols], start=True, stop=True)

        def open_q(k, s):
            q_stage[(k, s)] = ring3.tile([P, CHUNK, PACK], BF16, name="q_stage", tag="q_stage", align_bytes=64)

        def weave_q(k, s, width):
            nc.vector.tensor_tensor(
                out=q_stage[(k, s)][:, 0:width, :].rearrange("p (c i) t -> p c t i", i=2),
                in0=logits[k][:, :, s * CHUNK : s * CHUNK + width].rearrange("p t (c i) -> p c t i", i=2),
                in1=factor_bank[:, k * PACK : (k + 1) * PACK].unsqueeze(1).unsqueeze(3).to_broadcast([P, width // 2, PACK, 2]),
                op=ALU.mult,
            )

        def weave_q_rest(k, s, first):
            nc.gpsimd.tensor_tensor(
                out=q_stage[(k, s)][:, first:CHUNK, :],
                in0=logits[k][:, :, s * CHUNK + first : (s + 1) * CHUNK].rearrange("p t m -> p m t"),
                in1=factor[:, k * PACK : (k + 1) * PACK].unsqueeze(1).to_broadcast([P, CHUNK - first, PACK]),
                op=ALU.mult,
            )

        def quantize_q(k, s):
            cols = slice(s * CHUNK, (s + 1) * CHUNK)
            quantize(q_stage[(k, s)][:].rearrange("p m t -> p (m t)"), q_codes[:, k, cols], q_scales[:, k, cols])

        def gather(j, k):
            if k == 0:
                accs[j] = bank(ACC_BANK[j])
            rows = slice(j * P, (j + 1) * P)
            nc.tensor.matmul_mx(
                out=accs[j][:],
                lhsT=q_codes[:, k, rows].bitcast(FP8X4),
                lhsT_scale=q_scales[:, k, rows],
                rhs=z_codes[:, k, :].bitcast(FP8X4),
                rhs_scale=z_scales[:, k, :],
                start=(k == 0),
                stop=(k == GROUPS - 1),
            )

        def half(n):
            if n >= 2 * TILES:
                return
            if n % 8 == 0 and n > 0:
                open_group(n // 8)
            add_bias(n // 2, n % 2)
            if n + 2 < 2 * TILES:
                score(n // 2 + 1, n % 2)

        factor_bank = bank(4)
        gain_bank = factor_bank[:, TILES : 2 * TILES]
        keep_warm(factor_bank, 4)
        turn(("x", 0), x_raw[0], 5)
        turn(("y", 0), y_raw[0], 6)
        b_banks = []
        for h in range(2):
            acc = bank(h)
            nc.tensor.matmul(out=acc[:], lhsT=ones[:, 0:P], rhs=b_row[:, h * HALF : (h + 1) * HALF], start=True, stop=True)
            b_banks.append(acc)
            turn(("y", 1 + h), y_raw[1 + h], [7, 2][h])
        turn(("y", 3), y_raw[3], 3)
        spill(("x", 0), "scalar")
        keep_warm(factor_bank, 1)
        turn(("x", 1), x_raw[1], 5)
        spill(("y", 0), "vector")
        quantize_x(0)
        nc.scalar.copy(out=b_all[:, 0:HALF], in_=b_banks[0][:])
        quantize_y(0)
        spill(("y", 1), "vector")
        nc.scalar.copy(out=b_all[:, HALF:M], in_=b_banks[1][:])
        spill(("y", 2), "scalar")
        quantize_y(1)
        score(0, 0)
        keep_warm(factor_bank, 1)
        spill(("y", 3), "scalar")
        quantize_y(2)
        open_group(0)
        quantize_y(3)
        spill(("x", 1), "scalar")
        score(0, 1)
        nc.scalar.activation(out=gain[:], in_=g_sb[:].rearrange("p g t -> p (g t)"), func=ACT.Copy, scale=float(M))
        open_z(0)
        for s in range(4):
            weave_z(0, 2 * s, 2, "gpsimd")

        mass_banks = [bank(2), bank(3)]

        for i in range(TILES - 1):
            if i >= 6 and i % 4 == 2:
                spread_factor((i - 6) // 4)
            for h in range(2):
                half(2 * i + LEAD[i] + h)
                if i == 0 and h == 0:
                    turn(("x", 2), x_raw[2], 6)
            soft_exp(i)
            if i >= 1:
                exp_tile(i - 1)
            make_shift(i)
            if i in (2, 9, 13):
                quantize_z({2: 0, 9: 1, 13: 2}[i])
            if i >= EARLY_INVERT:
                invert(i - 2)
            if i in SPILL_ON_SCALAR:
                spill(("x", SPILL_ON_SCALAR[i]), "scalar")
            if i < 7 and i + 1 not in SPILL_ON_SCALAR.values():
                quantize_x(i + 1)
            if i - 1 in SPILL_ON_SCALAR:
                quantize_x(SPILL_ON_SCALAR[i - 1])
            if LEAD[i + 1] > LEAD[i]:
                half(2 * i + 2 + LEAD[i])
            if i < 5:
                turn(("x", i + 3), x_raw[i + 3], 5 + (i + 2) % 3)
            for late in MASS_AT.get(i, ()):
                mass_terms(late, 0)
                mass_terms(late, 1)
            if i >= 8 and i % 4 < 3:
                gather(i % 4, (i - 8) // 4)
            if i < 3:
                keep_warm(factor_bank, 1)
            if i == 2:
                nc.tensor.matmul(out=gain_bank, lhsT=ident[:], rhs=gain[:], start=True, stop=True)
            if i in (6, 7, 11, 14):
                add_nothing(0)
            if i >= 7:
                quantize_q((i - 7) // 4, (i - 7) % 4)
            if 2 <= i < EARLY_INVERT:
                invert(i - 2)
            if i >= 2:
                normalise(i - 2, "gpsimd")
            if i >= 2:
                first, count = (i - 2, 1) if i < 6 else (2 * i - 8, 2)
                if first % 8 == 0:
                    open_z(1 + first // 8)
                weave_z(1 + first // 8, first % 8, count, "gpsimd")
            if i < 6 and i + 2 not in SPILL_ON_SCALAR.values():
                spill(("x", i + 2), "vector")
            if i >= 6:
                k, s = divmod(i - 6, 4)
                open_q(k, s)
                weave_q(k, s, CHUNK)
            if i >= 5 and i % 4 == 1:
                make_factor((i - 5) // 4)

        weave_z(3, 6, 1, "scalar")
        soft_exp(15)
        exp_tile(14)
        make_shift(15)
        weave_z(3, 7, 1, "scalar")
        exp_tile(15)
        open_q(2, 1)
        weave_q(2, 1, CHUNK)
        gather(3, 0)
        gather(3, 1)
        add_nothing(0)
        mass_terms(12, 0)
        mass_terms(12, 1)
        gather(4, 0)
        gather(4, 1)
        quantize_q(2, 0)
        invert(13)
        quantize_q(2, 1)
        normalise(13, "gpsimd")
        gather(0, 2)
        gather(1, 2)
        open_q(2, 2)
        weave_q(2, 2, CHUNK)
        invert(14)
        normalise(14, "scalar")
        open_q(2, 3)
        weave_q(2, 3, CHUNK)
        add_nothing(0)
        add_nothing(1)
        mass_terms(13, 0)
        mass_terms(13, 1)
        gather(2, 2)
        gather(3, 2)
        invert(15)
        normalise(15, "scalar")
        quantize_z(3)
        make_factor(3)
        quantize_q(2, 2)
        quantize_q(2, 3)
        spread_factor(3)
        mass_terms(14, 0)
        mass_terms(14, 1)
        add_nothing(1)
        mass_terms(15, 0)
        mass_terms(15, 1)
        gather(4, 2)
        open_q(3, 3)
        weave_q_rest(3, 3, LAST_SPLIT)
        for s in (0, 1):
            open_q(3, s)
            weave_q(3, s, CHUNK)
        weave_q(3, 3, LAST_SPLIT)

        pairs = {}
        weighted = {}
        results = {}
        rounded = {}
        r_turned = {}
        r_stage = {}

        def weigh(j):
            n = PAIR_ORDER.index(j)
            if n // 2 not in pairs:
                pairs[n // 2] = ring3.tile([P, 2, C], F32, name="weighted", tag="posterior")
            t = pairs[n // 2][:, n % 2, :]
            if j in WEIGH_ON_SCALAR:
                nc.scalar.activation(out=t, in_=v_raw[:, j, :], func=ACT.Copy, scale=mass[:, j : j + 1])
            else:
                nc.gpsimd.tensor_scalar(
                    out=t, in0=v_raw[:, j, :], scalar1=mass[:, j : j + 1], scalar2=0.0, op0=ALU.mult, op1=ALU.add
                )
            weighted[j] = t

        def finish(j):
            t = ring4.tile([P, C], F32, name="result", tag="result", bufs=M_TILES)
            nc.vector.scalar_tensor_tensor(
                out=t[:], in0=accs[j][:], scalar=1.0 / math.sqrt(N), in1=weighted[j], op0=ALU.mult, op1=ALU.subtract
            )
            nc.sync.dma_start(out=out_0[j * P : (j + 1) * P, :], in_=t[:])
            results[j] = t

        def round_result(j):
            t = ring4.tile([P, C], BF16, name="rounded", tag="rounded", align_bytes=64)
            dst = t[:].rearrange("p (u j e) -> p u j e", u=2, e=2)
            src = results[j][:].rearrange("p (j u e) -> p u j e", u=2, e=2)
            if j in ROUND_ON_VECTOR:
                nc.vector.tensor_copy(out=dst, in_=src)
            else:
                nc.scalar.copy(out=dst, in_=src)
            rounded[j] = t

        def turn_result(j):
            acc = bank(ACC_BANK[j])
            words = rounded[j][:].bitcast(F32)
            for u in range(2):
                nc.tensor.transpose(acc[:, u * P : (u + 1) * P], words[:, u * P : (u + 1) * P], ident[:])
            r_turned[j] = acc

        def spill_result(j):
            t = ring4.tile([P, C], BF16, name="r_stage", tag="r_stage", align_bytes=64, bufs=M_TILES)
            nc.scalar.copy(
                out=t[:].bitcast(F32).rearrange("p (r u) -> p r u", u=2),
                in_=r_turned[j][:, 0 : 2 * P].rearrange("p (u r) -> p r u", u=2),
            )
            r_stage[j] = t

        words_out = out_1[0].rearrange("p m t -> p (m t)").bitcast(I32)

        def quantize_result(j):
            cols = slice(j * P, (j + 1) * P)
            quantize(r_stage[j][:], r_codes[:, cols], r_scales[:, cols])
            if j % 2 == 1:
                pair = slice((j - 1) * P, (j + 1) * P)
                nc.sync.dma_start(out=words_out[:, pair], in_=r_codes[:, pair].bitcast(I32))

        for j in range(M_TILES):
            sum_mass(j)
        for j in WEIGH_ON_SCALAR:
            weigh(j)
        gather(5, 0)
        gather(5, 1)
        quantize_q(3, 0)
        gather(0, 3)
        gather(1, 3)
        gather(6, 0)
        gather(6, 1)
        quantize_q(3, 3)
        quantize_q(3, 1)
        gather(2, 3)
        gather(3, 3)
        gather(5, 2)
        gather(6, 2)
        gather(6, 3)
        open_q(3, 2)
        weave_q_rest(3, 2, THIRD_SPLIT)
        weave_q(3, 2, THIRD_SPLIT)
        finish(0)
        finish(1)
        for j in (4, 5, 7):
            weigh(j)
        gather(7, 0)
        gather(7, 1)
        round_result(0)
        quantize_q(3, 2)
        finish(2)
        gather(7, 2)
        gather(4, 3)
        gather(5, 3)
        gather(7, 3)
        turn_result(0)
        round_result(1)
        turn_result(1)
        for n in range(3, M_TILES):
            finish(FINISH_ORDER[n])
            j = FINISH_ORDER[n - 1]
            if j not in ROUND_ON_VECTOR:
                round_result(j)
                turn_result(j)
            if n >= 4:
                spill_result(FINISH_ORDER[n - 4])
        for j in ROUND_ON_VECTOR:
            round_result(j)
            turn_result(j)
        for n, j in enumerate(FINISH_ORDER):
            if n >= 4:
                spill_result(j)
            quantize_result(j)
        scales_out = out_2[0].bitcast(I32)
        for s in range(4):
            queue = nc.scalar if s % 2 else nc.sync
            queue.dma_start(out=scales_out[4 * s : 4 * s + 4, :], in_=r_scales[32 * s : 32 * s + 4, :].bitcast(I32))
